import numpy as np, ml_dtypes
CORES = [3,7,11,15,131,135,139,143]
N = 8
import mx_ref
BF = ml_dtypes.bfloat16
def cols(t, e):
    v = np.concatenate([t.reshape(128, -1, 4), np.zeros((128, 1, 4), BF)], axis=1)
    return np.ascontiguousarray(v[:, e]).reshape(128, -1)
def cut(t, i, w=512):
    return t[:, w * i:w * i + w]
def f(rng, *shape):
    return mx_ref.flush((rng.standard_normal(shape, dtype=np.float32) * np.exp2(rng.integers(-2, 3, shape[:-1] + (1,)))).astype(BF))
def wide(rng, *shape, cols=0):
    v = rng.standard_normal(shape, dtype=np.float32) * np.exp2(rng.integers(-12, 13, shape)).astype(np.float32)
    if cols: v *= np.repeat(np.exp2(rng.integers(-cols, cols + 1, shape[:-2] + (1, shape[-1] // 4))) * (rng.random(shape[:-2] + (1, shape[-1] // 4)) > 0.0625), 4, axis=-1).astype(np.float32)
    return mx_ref.flush(v.astype(BF))
P, K, R, O = 128, 32, 5, 2
PART = [1, 2, 4, 1, 2]
def scores(c, qt):
    k = mx_ref.quantize(np.concatenate([qt[r][:, :4 * R] for r in range(N)], axis=1))
    s = [mx_ref.matmul(mx_ref.quantize(cut(c[q], i)), k) for q in range(N) for i in range(P // 128)]
    return np.concatenate(s).reshape(N * P, N, R)
def play(s):
    held, use, out = np.arange(N * P).reshape(N, P), np.zeros((N, P), np.float32), []
    for t in range(R):
        left = []
        for r in range(N):
            v = s[held[r], r, t]
            use[r] = use[r] + v * v
            left.append(np.argsort(use[r], kind="stable")[:K])
        new = held.copy()
        for r in range(N):
            p = r ^ PART[t]
            new[r, left[r]] = held[p, left[p]]
            use[r, left[r]] = 0
        held = new
        out.append(held)
    return np.stack(out)
def fit(s):
    a = np.abs(s)
    return bool(np.isfinite(a).all() and ((a == 0) | (a >= 2.0 ** -60) & (a <= 2.0 ** 60)).all())
def times(t, v):
    return mx_ref.flush((t.astype(np.float32) * np.asarray(v, np.float32)).astype(BF))
def plain(rng):
    q = np.array(f(rng, N, 128, 512))
    q[:, :, 4 * R:] = 0
    return {"c": f(rng, N, 128, 4 * P), "qt": q, "w": f(rng, N, 128, 512 * O)}
def first(make, good=None):
    for i in range(50):
        d = make()
        s = scores(d["c"], d["qt"])
        if fit(s) and (good is None or good(s)): return d
    raise RuntimeError("no draw of 50 is fit")
def athome(s):
    h, a = play(s), np.ones((N, R + 1, P), bool)
    for r in range(N):
        for t in range(R): a[r, t + 1] = np.isin(np.arange(P * r, P * r + P), h[t, r])
    return a
def setup_inputs(rng):
    return first(lambda: plain(rng))
def setup_inputs_sides(rng):
    top = np.arange(128) < 64
    def make():
        d = plain(rng)
        half = np.stack([rng.permutation(P) < P // 2 for r in range(N)])
        d["c"] = times(d["c"], np.repeat(half[:, None, :] == top[None, :, None], 4, axis=2))
        for t in range(R):
            g = np.where(top == (PART[t] == 1), 1.0, 2.0 ** -6) * 4.0 ** t
            d["qt"][:, :, 4 * t:4 * t + 4] = times(d["qt"][:, :, 4 * t:4 * t + 4], g[None, :, None])
        return d
    def good(s):
        a = athome(s)
        return bool((~a[:, :-1] & a[:, 1:]).any(axis=(1, 2)).all())
    return first(make, good)
def setup_inputs_ties(rng):
    def make():
        d = plain(rng)
        d["c"] = np.stack([times(cols(d["c"][r], rng.integers(0, 6, P)), np.repeat(1 - 2 * rng.integers(0, 2, P), 4)) for r in range(N)])
        return d
    def good(s):
        for r in range(N):
            v = s[P * r:P * r + P, r, 0]
            u = np.sort(v * v)
            if u[K - 1] != u[K]: return False
        return True
    return first(make, good)
def setup_inputs_shrink(rng):
    low = np.arange(N) >= N - N // 4
    def make():
        d = plain(rng)
        size = np.exp2(np.where(low, -30.0, 23.0)[:, None] + 2 * rng.random((N, P))) * (1 - 2 * rng.integers(0, 2, (N, P)))
        d["c"] = ((1 + rng.random((N, 128, 4 * P))) * np.repeat(size, 4, axis=1)[:, None, :]).astype(np.float32).astype(BF)
        on = ~low[:, None] | np.stack([rng.permutation(128) < 2 for r in range(N)])
        for t in range(R):
            g = np.exp2(np.where(low, 8.0 * (R - 1 - t) - 30.0, 21.0 - 8.0 * t))
            d["qt"][:, :, 4 * t:4 * t + 4] = ((1 + rng.random((N, 128, 4))) * (g[:, None] * on)[:, :, None]).astype(np.float32).astype(BF)
        return d
    def good(s):
        h, a, b = play(s), np.zeros(N, bool), np.zeros(N, bool)
        for r in range(N):
            at, use, since = np.arange(P * r, P * r + P), np.zeros(P, np.float32), np.zeros(P, int)
            if low[r] and np.abs(s[at, r, R - 1]).max() > 2.0 ** -50 or not low[r] and np.abs(s[at, r, 0]).min() < 2.0 ** 50: return False
            for t in range(R):
                v = s[at, r]
                use = use + v[:, t] * v[:, t]
                sums = np.concatenate([np.zeros((P, 1), np.float32), np.cumsum(v * v, axis=1)], axis=1)
                diff = sums[:, t + 1] - sums[np.arange(P), since]
                a[r] |= (np.argsort(use, kind="stable")[:K] != np.argsort(diff, kind="stable")[:K]).any()
                b[r] |= np.sort(use)[K - 1] > 1e30
                moved = h[t, r] != at
                at = h[t, r]
                use[moved] = 0
                since[moved] = t + 1
        return bool(2 * a.sum() > N and 2 * b.sum() > N)
    return first(make, good)
def setup_inputs_turn(rng):
    on = (np.arange(128) // (128 // N))[None, :] == np.arange(N)[:, None]
    def make():
        d = plain(rng)
        d["c"] = times(d["c"], np.where(on, 2.0 ** -8, 1.0)[:, :, None])
        d["qt"] = times(d["qt"], on[:, :, None])
        return d
    return first(make, lambda s: bool((~athome(s)).any(axis=1).all()))
def setup_inputs_spread(rng):
    return first(lambda: {**plain(rng), "c": wide(rng, N, 128, 4 * P, cols=6)})
def check_inputs(d):
    b = []
    for k in ("c", "qt", "w"):
        v = np.abs(d[k].astype(np.float32))
        if not (np.isfinite(v).all() and ((v == 0) | (v >= 2.0 ** -30) & (v <= 2.0 ** 30)).all()): b.append("a value of " + k)
    if (d["qt"][:, :, 4 * R:].astype(np.float32) != 0).any(): b.append("qt has numbers behind its first R columns")
    if not b and not fit(scores(d["c"], d["qt"])): b.append("a score")
    return b
def reference(c, qt, w):
    held = play(scores(c, qt))
    every = np.concatenate([c[q] for q in range(N)], axis=1)
    y = np.zeros((N, 128, R * O * P), np.float32)
    for r in range(N):
        u, at = np.unique(held[:, r].reshape(-1), return_inverse=True)
        at = at.reshape(R, P)
        q = mx_ref.quantize(cols(every, np.concatenate([u, np.full(-len(u) % 4, -1)])))
        for o in range(O):
            z = mx_ref.matmul(mx_ref.quantize(cut(w[r], o)), q)
            for t in range(R):
                i = (t * O + o) * P
                y[r, :, i:i + P] = z[:, at[t]]
    return {"y": y}

@@ -1,0 +1,393 @@
+from concourse.mybir import dt, AluOpType, AxisListType, ActivationFunctionType
+
+P, K, R, O = 128, 32, 5, 2
+PREV = 1.0 - 2.0 ** -24
+TINY = 2.0 ** -121
+
+F4, BF, I32, U16, CODE, PLANE = "float32", "bfloat16", "int32", "uint16", "float8_e4m3fn_x4", "uint8"
+WW = [128, 160, 192, 224, 256, 160]
+SCRATCH = {
+    "cb": ("sbuf", [128, 512], BF), "qb": ("sbuf", [128, 20], BF), "wb": ("sbuf", [128, 1024], BF),
+    "rb": ("sbuf", [128, 2560], BF), "rq": ("sbuf", [128, 640], CODE), "rs": ("sbuf", [128, 640], PLANE),
+    "wq": ("sbuf", [128, 256], CODE), "ws": ("sbuf", [128, 256], PLANE),
+    "qrow": ("sbuf", [128, 128], F4), "q32": ("sbuf", [128, 128], F4), "pt": ("sbuf", [128, 128], F4),
+    "fd": ("sbuf", [128, 128], F4), "j3": ("sbuf", [128, 2, 32], F4), "js": ("sbuf", [128, 2, 32], F4),
+    "ptb": ("sbuf", [128, 128], BF), "b32": ("sbuf", [128, 4], F4), "ones": ("sbuf", [128, 128], BF),
+    "zeros": ("sbuf", [128, 128], BF), "rm": ("sbuf", [128, 512], BF), "rmc": ("sbuf", [128, 96], BF),
+    "half": ("sbuf", [128, 32], F4), "big": ("sbuf", [128, 32], F4),
+    "sq": ("sbuf", [128, 640], F4), "kk": ("sbuf", [128, 640], F4), "sv": ("sbuf", [128, 128], F4),
+    "km": ("sbuf", [128, 128], F4), "kt": ("sbuf", [128, 128], F4), "kd": ("sbuf", [128, 128], F4),
+    "cm": ("sbuf", [128, 512], BF), "cs": ("sbuf", [128, 512], BF),
+    "hb": ("sbuf", [128, 2, 128], BF), "ht": ("sbuf", [128, 2, 128], BF),
+    "lbf": ("sbuf", [128, 10], F4), "lbu": ("sbuf", [128, 10], U16),
+    "bs": ("sbuf", [128, 32], F4), "pp": ("sbuf", [128, 64], F4), "pac": ("sbuf", [128, 32], F4),
+    "ff": ("sbuf", [128, 64], F4), "xm": ("sbuf", [128, 64], F4), "svb": ("sbuf", [128, 32], F4),
+    "svc": ("sbuf", [128, 32], F4), "avt": ("sbuf", [128, 32], F4), "av": ("sbuf", [128, 32], F4),
+    "avc": ("sbuf", [128, 32], F4), "af": ("sbuf", [128, 32 * 25], F4), "asum": ("sbuf", [128, 32], F4),
+    "xa": ("sbuf", [128, 32], F4), "at": ("sbuf", [128, 32], F4), "gm": ("sbuf", [128, 96], BF),
+    "gs": ("sbuf", [128, 96], F4), "hc": ("sbuf", [128, 2, 64], F4), "hd": ("sbuf", [128, 2, 64], F4),
+    "plf": ("sbuf", [128, 10], F4), "plu": ("sbuf", [128, 10], U16), "pls": ("sbuf", [128, 2], F4),
+    "pld": ("sbuf", [128, 2], F4), "lpu": ("sbuf", [128, 10], U16),
+    "zl": ("sbuf", [128, 256], F4), "zf": ("sbuf", [128, 64], F4), "yy": ("sbuf", [128, 256 * 6], F4),
+    "ps": ("psum", [128, 4096], F4),
+}
+for _t in range(6):
+    SCRATCH["win%d" % _t] = ("sbuf", [128, WW[_t]], CODE)
+    SCRATCH["wis%d" % _t] = ("sbuf", [128, WW[_t]], PLANE)
+for _t in range(5):
+    SCRATCH["out%d" % _t] = ("sbuf", [128, 32], CODE)
+    SCRATCH["ous%d" % _t] = ("sbuf", [128, 32], PLANE)
+DSEM = ["dc", "dq", "dw"] + ["dn%d" % t for t in range(1, 6)] + ["dg%d" % t for t in range(2, 5)] + ["dy%d" % t for t in range(6)]
+SEMAPHORES = ["cv", "ca", "ct", "cg"] + DSEM + ["arr%d" % t for t in range(5)] + ["snd%d" % t for t in range(5)]
+
+
+def rank_program(g, core, T, topo):
+    rank = T.rank_of(core)
+    if rank is None:
+        return
+    A, F = AluOpType, ActivationFunctionType
+    eng = {"v": g.vector, "a": g.scalar, "t": g.tensor, "g": g, "s": g.sync}
+    csem = {"v": "cv", "a": "ca", "t": "ct", "g": "cg"}
+    count = {"v": 0, "a": 0, "t": 0, "g": 0}
+    known = {q: {} for q in eng}
+    snap = {}
+    wr, rd = {}, {}
+    ends = {}
+
+    def wait(q, sem, val):
+        if known[q].get(sem, 0) >= val:
+            return
+        eng[q].wait_ge(T.sem[sem], val)
+        known[q][sem] = val
+        for s, v in snap.get((sem, val), {}).items():
+            if known[q].get(s, 0) < v:
+                known[q][s] = v
+
+    def waits(q, reads, writes):
+        need = {}
+        for (n, lo, hi) in reads:
+            for (l, h, q2, s, v) in wr.get(n, ()):
+                if l < hi and lo < h:
+                    need[s] = max(need.get(s, 0), v)
+        for (n, lo, hi) in writes:
+            for (l, h, q2, s, v) in wr.get(n, ()):
+                if l < hi and lo < h:
+                    need[s] = max(need.get(s, 0), v)
+            for (l, h, q2, s, v) in rd.get(n, ()):
+                if l < hi and lo < h and (q2 != q or s[0] == "d"):
+                    need[s] = max(need.get(s, 0), v)
+        for s in sorted(need):
+            wait(q, s, need[s])
+
+    def note(q, reads, writes, sem, val):
+        snap[(sem, val)] = dict(known[q])
+        for (n, lo, hi) in writes:
+            wr[n] = [e for e in wr.get(n, ()) if not (lo <= e[0] and e[1] <= hi)] + [(lo, hi, q, sem, val)]
+            rd[n] = [e for e in rd.get(n, ()) if not (lo <= e[0] and e[1] <= hi)]
+        for (n, lo, hi) in reads:
+            rd.setdefault(n, []).append((lo, hi, q, sem, val))
+
+    def op(q, fn, reads, writes):
+        waits(q, reads, writes)
+        ins = fn()
+        count[q] += 1
+        ins.then_inc(T.sem[csem[q]], 1)
+        note(q, reads, writes, csem[q], count[q])
+
+    def dma(q, sem, *moves):
+        for (out, in_, reads, writes) in moves:
+            waits(q, reads, writes)
+            eng[q].dma_start(out, in_).then_inc(T.sem[sem], 16)
+        ends[sem] = 16 * len(moves)
+        for (out, in_, reads, writes) in moves:
+            note(q, reads, writes, sem, ends[sem])
+
+    def V(n, a, b, step=1):
+        return (T[n][:, a:b] if step == 1 else T[n][:, a:b:step], [(n, a, b)])
+
+    def V3(n, a, b):
+        return (T[n][:, :, a:b], [(n, a, b)])
+
+    def H(n, j, a, b):
+        return (T[n][:, j, a:b], [(n, a, b)])
+
+    def IX(v, off):
+        return (v[0].indirect(off[0]), v[1] + off[1])
+
+    def C32(v):
+        return (v[0].bitcast(dt.uint32), v[1])
+
+    def ap(x):
+        return x[0] if isinstance(x, tuple) else x
+
+    def rg(*xs):
+        r = []
+        for x in xs:
+            if isinstance(x, tuple):
+                r += x[1]
+        return r
+
+    def ts(out, i0, s1, op0, s2=None, op1=None):
+        if op1 is None:
+            op("v", lambda: g.vector.tensor_scalar(ap(out), ap(i0), ap(s1), None, op0), rg(i0, s1), rg(out))
+        else:
+            op("v", lambda: g.vector.tensor_scalar(ap(out), ap(i0), ap(s1), ap(s2), op0, op1), rg(i0, s1, s2), rg(out))
+
+    def tt(out, i0, i1, o):
+        op("v", lambda: g.vector.tensor_tensor(ap(out), ap(i0), ap(i1), o), rg(i0, i1), rg(out))
+
+    def cp(out, in_):
+        op("v", lambda: g.vector.tensor_copy(ap(out), ap(in_)), rg(in_), rg(out))
+
+    def scatter(win, off, vals):
+        op("v", lambda: g.vector.tensor_copy(win[0].indirect(off[0]), ap(vals)), rg(off, vals), rg(win))
+
+    def tr(out, in_):
+        op("v", lambda: g.vector.transpose(ap(out), ap(in_)), rg(in_), rg(out))
+
+    def add_up(out, in_):
+        op("v", lambda: g.vector.tensor_reduce(ap(out), ap(in_), AxisListType.X, A.add), rg(in_), rg(out))
+
+    def scan(out, d0, d1):
+        op("v", lambda: g.vector.tensor_tensor_scan(ap(out), ap(d0), ap(d1), 0.0, A.mult, A.add), rg(d0, d1), rg(out))
+
+    def fill(v, c):
+        op("v", lambda: g.vector.memset(ap(v), c), [], rg(v))
+
+    def quant(q, s, a, b, in_):
+        x, y = V(q, a, b), V(s, a, b)
+        op("v", lambda: g.vector.quantize_mx(x[0], y[0], ap(in_)), rg(in_), rg(x, y))
+
+    def act(out, in_, f, **kw):
+        op("a", lambda: g.scalar.activation(ap(out), ap(in_), f, **{k: ap(kw[k]) for k in kw}), rg(in_, *kw.values()), rg(out))
+
+    bank = [0]
+
+    def mm(lq, ls, la, rq, rs, ra):
+        b = 512 * (bank[0] % 8)
+        bank[0] += 1
+        l, m, r, s = V(lq, la, la + 128), V(ls, la, la + 128), V(rq, ra, ra + 128), V(rs, ra, ra + 128)
+        op("t", lambda: g.tensor.matmul_mx(T.ps[:, b:b + 128], l[0], m[0], r[0], s[0], True, True), rg(l, m, r, s), [("ps", b, b + 512)])
+        return b
+
+    def PS(b, lo, hi):
+        return (T.ps[:, b + lo:b + hi], [("ps", b, b + 512)])
+
+    def iota(v, pattern, mult):
+        if SCRATCH[v[1][0][0]][2] == F4:
+            op("g", lambda: g.iota(v[0], pattern, 0, mult, allow_small_or_imprecise_dtypes=True), [], v[1])
+        else:
+            op("g", lambda: g.iota(v[0], pattern, 0, mult), [], v[1])
+
+    dma("a", "dq", (T.qb[:, 0:20], T.qt[:, 0:20], [], [("qb", 0, 20)]))
+    dma("s", "dc", (T.cb[:, 0:512], T.c[:, 0:512], [], [("cb", 0, 512)]))
+    dma("s", "dw", (T.wb[:, 0:1024], T.w[:, 0:1024], [], [("wb", 0, 1024)]))
+    iota(V("qrow", 0, 128), [[1, 128]], 0)
+    iota(V("q32", 0, 128), [[0, 4], [1, 32]], 0)
+    J3, JS = (T.j3[:, :, :], [("j3", 0, 32)]), (T.js[:, :, :], [("js", 0, 32)])
+    iota(J3, [[16, 2], [0, 2], [1, 16]], 0)
+    fill(V("zeros", 0, 128), 0.0)
+    fill(V("ones", 0, 128), 1.0)
+    fill(V("rm", 0, 512), 1.0)
+    for m in range(4):
+        fill(V("rm", 128 * m, 128 * m + 1), 0.0)
+    tr(V("pt", 0, 128), V("qrow", 0, 128))
+    cp(V("ptb", 0, 128), V("pt", 0, 128))
+    ts(V("fd", 0, 128), V("q32", 0, 128), V("pt", 0, 1), A.is_ge, PREV, A.max)
+    fill(V("half", 0, 32), 2.0 ** 63)
+    tt(V("big", 0, 32), V("half", 0, 32), V("half", 0, 32), A.mult)
+
+    def rep(t, e, on):
+        o, q = V("rb", 512 * t + e, 512 * t + 512, 4), V("qb", 4 * t + e, 4 * t + e + 1)
+        if on == "v":
+            ts(o, V("ones", 0, 128), q, A.mult)
+        else:
+            act(o, V("zeros", 0, 128), F.Identity, bias=q)
+
+    def square(dst, b, lo, hi):
+        act(dst, PS(b, lo, hi), F.Square)
+
+    def move(m, n, a, b):
+        x, y, s, r = V("win%d" % n, a, b), V("win%d" % m, a, b), V("wis%d" % n, a, b), V("wis%d" % m, a, b)
+        return ((x[0].bitcast(dt.uint8), y[0].bitcast(dt.uint8), y[1], x[1]), (s[0], r[0], r[1], s[1]))
+
+    def SQ(t):
+        return V("sq", 128 * t, 128 * t + 128)
+
+    def KK(t):
+        return V("kk", 128 * t, 128 * t + 128)
+
+    def LB(t):
+        return V("lbu", 2 * t, 2 * t + 2)
+
+    def LP(t):
+        return LB(0) if t == 0 else V("lpu", 2 * t, 2 * t + 2)
+
+    def rank32(k, t):
+        ts(V("km", 0, 128), k, TINY, A.max)
+        tr(V("kt", 0, 128), V("km", 0, 128))
+        tt(V("kd", 0, 128), V("km", 0, 128), V("fd", 0, 128), A.mult)
+        for m in range(4):
+            u, c, d = V("kt", 32 * m, 32 * m + 1), 128 * m, 32 * m
+            if m > 0:
+                ts(V("cm", c, c + d), V("km", 0, d), u, A.is_le)
+            if m < 3:
+                ts(V("cm", c + d + 32, c + 128), V("km", d + 32, 128), u, A.is_lt)
+        for m in range(4):
+            u, c, d = V("kt", 32 * m, 32 * m + 1), 128 * m, 32 * m
+            ts(V("cm", c + d, c + d + 32), V("kd", d, d + 32), u, A.is_lt)
+        scan(V("cs", 0, 512), V("rm", 0, 512), V("cm", 0, 512))
+        for m in range(4):
+            ts(V3("hb", 32 * m, 32 * m + 32), J3, V("cs", 128 * m + 127, 128 * m + 128), A.is_equal,
+               V("ptb", 32 * m, 32 * m + 1), A.mult)
+        for j in range(2):
+            tr(H("ht", j, 0, 128), H("hb", j, 0, 128))
+        for j in range(2):
+            add_up(V("lbf", 2 * t + j, 2 * t + j + 1), H("ht", j, 0, 128))
+        cp(LB(t), V("lbf", 2 * t, 2 * t + 2))
+
+    def send(t):
+        d = T.cores[rank ^ [1, 2, 4, 1, 2][t]]
+        rid, pid = topo.addr(d, core)
+        es = topo.engines(core, d)[:8]
+        mask, n = sum(1 << e for e in es), len(es)
+        a = 128 + 32 * t if t < 4 else 128
+        o, s = V("out%d" % t, 0, 32), V("ous%d" % t, 0, 32)
+        waits("g", rg(o), [])
+        g.remote_dma(T["win%d" % (t + 1)][:, a:a + 32].bitcast(dt.uint8), o[0].bitcast(dt.uint8),
+                     T.sem["arr%d" % t], T.sem["snd%d" % t], pid, rid, mask)
+        waits("g", rg(s), [])
+        g.remote_dma(T["wis%d" % (t + 1)][:, a:a + 32], s[0], T.sem["arr%d" % t], T.sem["snd%d" % t], pid, rid, mask)
+        ends["snd%d" % t] = ends["arr%d" % t] = 2 * n
+        for nm in ("win%d" % (t + 1), "wis%d" % (t + 1)):
+            wr.setdefault(nm, []).append((a, a + 32, "x", "arr%d" % t, 2 * n))
+
+    def pick(t, off):
+        o, s = V("out%d" % t, 0, 32), V("ous%d" % t, 0, 32)
+        w = WW[t]
+        cp(C32(o), IX(C32(V("win%d" % t, 0, w)), off))
+        act(s, IX(V("wis%d" % t, 0, w), off), F.Copy)
+        send(t)
+
+    def stays(t):
+        pa = V("pp", 32, 64)
+        act(pa, IX(V("qrow", 0, 128), LP(t - 1)), F.Copy)
+        act(V("avt", 0, 32), pa, F.Identity, scale=1.0 / 256, bias=float(128 + 32 * (t - 1)))
+        rank32(KK(t), t)
+        act(V("pp", 0, 32), IX(V("qrow", 0, 128), LB(t)), F.Copy)
+        act(V("svb", 0, 32), IX(V("sv", 0, 128), LB(t)), F.Copy)
+        tr(V("pac", 0, 32), pa)
+        cp(V("bs", 0, 32), IX(V("km", 0, 128), LB(t)))
+        tt(V("av", 0, 32), V("avt", 0, 32), V("qrow", 0, 32), A.add)
+        ts(V("ff", 0, 64), V("pp", 0, 64), V("pac", 0, 1), A.is_ge, PREV, A.max)
+        tt(V("xm", 0, 32), V("bs", 0, 32), V("ff", 0, 32), A.mult)
+        tr(V("avc", 0, 32), V("av", 0, 32))
+        tr(V("svc", 0, 32), V("svb", 0, 32))
+
+    def AF(q, t):
+        i = 32 * (5 * t + q)
+        return V("af", i, i + 32)
+
+    def merge(t):
+        b = mm("rq", "rs", 128 * t, "win%d" % t, "wis%d" % t, 32 * t)
+        a = AF(t, t - 1)
+        square(a, b, 96, 128)
+        ts(V("xa", 0, 32), a, TINY, A.max)
+        tr(V("at", 0, 32), V("xa", 0, 32))
+        tt(V("xm", 32, 64), V("xa", 0, 32), V("ff", 32, 64), A.mult)
+        ts(V("gm", 0, 64), V("xm", 0, 64), V("at", 0, 1), A.is_lt)
+        tr(V("gm", 64, 96), V("gm", 0, 32))
+        scan(V("gs", 0, 96), V("rmc", 0, 96), V("gm", 0, 96))
+        ts(V3("hc", 0, 32), JS, V("gs", 95, 96), A.is_equal, V("svc", 0, 1), A.mult)
+        ts(V3("hc", 32, 64), J3, V("gs", 63, 64), A.is_equal, V("avc", 0, 1), A.mult)
+        for j in range(2):
+            tr(H("hd", j, 0, 64), H("hc", j, 0, 64))
+        for j in range(2):
+            add_up(V("plf", 2 * t + j, 2 * t + j + 1), H("hd", j, 0, 64))
+        cp(V("plu", 2 * t, 2 * t + 2), V("plf", 2 * t, 2 * t + 2))
+
+    def places(t):
+        cp(V("pls", 0, 2), V("plu", 2 * t, 2 * t + 2))
+        tt(V("pld", 0, 2), V("plf", 2 * t, 2 * t + 2), V("pls", 0, 2), A.subtract)
+        ts(LP(t), V("pld", 0, 2), 256.0, A.mult)
+
+    for e in range(4):
+        rep(0, e, "v")
+    quant("rq", "rs", 0, 128, V("rb", 0, 512))
+    for e in range(4):
+        rep(1, e, "a")
+    quant("win0", "wis0", 0, 128, V("cb", 0, 512))
+    b0 = mm("rq", "rs", 0, "win0", "wis0", 0)
+    square(V("sq", 0, 128), b0, 0, 128)
+    for t in range(1, 6):
+        dma("s", "dn%d" % t, *move(0, t, 0, 128))
+    quant("rq", "rs", 128, 256, V("rb", 512, 1024))
+    b1 = mm("rq", "rs", 128, "win0", "wis0", 0)
+    square(V("sq", 128, 256), b1, 0, 128)
+    for t in range(2, 5):
+        for e in range(4):
+            rep(t, e, "a")
+    rank32(SQ(0), 0)
+    pick(0, LB(0))
+    tt(KK(1), SQ(0), SQ(1), A.add)
+    ts(V("sv", 0, 128), V("qrow", 0, 128), 1.0 + 1.0 / 256, A.mult)
+    scatter(KK(1), LP(0), V("big", 0, 32))
+    stays(1)
+    fill(V("rmc", 0, 96), 1.0)
+    fill(V("rmc", 0, 1), 0.0)
+    fill(V("rmc", 64, 65), 0.0)
+    ts(V("b32", 0, 1), V("pt", 0, 1), 32.0, A.add)
+    ts(JS, J3, -1.0, A.mult, V("b32", 0, 1), A.add)
+    quant("rq", "rs", 256, 640, V("rb", 1024, 2560))
+    for t in range(2, 5):
+        b = mm("rq", "rs", 128 * t, "win0", "wis0", 0)
+        square(SQ(t), b, 0, 128)
+    scatter(V("sv", 0, 128), LP(0), V("av", 0, 32))
+    tt(KK(2), KK(1), SQ(2), A.add)
+
+    YB = lambda t, o: V("yy", 256 * t + 128 * o, 256 * t + 128 * o + 128)
+    for t in range(1, 5):
+        merge(t)
+        later = [mm("rq", "rs", 128 * q, "win%d" % t, "wis%d" % t, 32 * t) for q in range(t + 1, 5)]
+        if t < 4:
+            dma("s", "dg%d" % (t + 1), *move(t, t + 1, 128, 128 + 32 * t)) if t < 4 else None
+        for q in range(t + 1, 5):
+            square(AF(q, t - 1), later[q - t - 1], 96, 128)
+        pick(t, V("plu", 2 * t, 2 * t + 2))
+        places(t)
+        if t == 4:
+            break
+        tt(V("asum", 0, 32), AF(t, t - 1), AF(t + 1, t - 1), A.add)
+        scatter(KK(t + 1), LP(t - 1), V("asum", 0, 32))
+        scatter(KK(t + 1), LP(t), V("big", 0, 32))
+        stays(t + 1)
+        if t < 3:
+            for q in range(t + 2, 5):
+                scatter(SQ(q), LP(t - 1), AF(q, t - 1))
+            scatter(V("sv", 0, 128), LP(t), V("av", 0, 32))
+            tt(KK(t + 2), KK(t + 1), SQ(t + 2), A.add)
+
+    quant("wq", "ws", 0, 256, V("wb", 0, 1024))
+    for o in range(O):
+        b = mm("wq", "ws", 128 * o, "win0", "wis0", 0)
+        act(YB(1, o), PS(b, 0, 128), F.Copy)
+    for o in range(O):
+        b = mm("wq", "ws", 128 * o, "win4", "wis4", 128)
+        act(V("zl", 128 * o, 128 * o + 128), PS(b, 0, 128), F.Copy)
+    for t in range(4):
+        for o in range(O):
+            scatter(YB(t + 1, o), LP(t), V("zl", 128 * o + 32 * t, 128 * o + 32 * t + 32))
+            act(YB(t + 2, o), YB(t + 1, o), F.Copy)
+        dma("s", "dy%d" % t, (T.y[:, 256 * t:256 * t + 256], T.yy[:, 256 * t + 256:256 * t + 512],
+                              [("yy", 256 * t + 256, 256 * t + 512)], []))
+    bs = [mm("wq", "ws", 128 * o, "win5", "wis5", 32) for o in range(O)]
+    act(V("zf", 0, 32), PS(bs[0], 96, 128), F.Copy)
+    cp(V("zf", 32, 64), PS(bs[1], 96, 128))
+    for o in range(O):
+        scatter(YB(5, o), LP(4), V("zf", 32 * o, 32 * o + 32))
+        dma("s" if o == 0 else "a", "dy%d" % (4 + o), (T.y[:, 1024 + 128 * o:1152 + 128 * o],
+            T.yy[:, 1280 + 128 * o:1408 + 128 * o], YB(5, o)[1], []))
+    for q in ("v", "a", "t", "g"):
+        wait("g", csem[q], count[q])
+    for s in sorted(ends):
+        wait("g", s, ends[s])

@@ -1,3 +1,4 @@
+from concourse.bass import DstId, RemoteDMATransfer
 from concourse.mybir import dt, AluOpType, AxisListType, ActivationFunctionType
 
 P, K, R, O = 128, 32, 5, 2
@@ -6,38 +7,30 @@ TINY = 2.0 ** -121
 
 F4, BF, I32, U16, CODE, PLANE = "float32", "bfloat16", "int32", "uint16", "float8_e4m3fn_x4", "uint8"
 WW = [128, 160, 192, 224, 256, 160]
-SCRATCH = {
-    "cb": ("sbuf", [128, 512], BF), "qb": ("sbuf", [128, 20], BF), "wb": ("sbuf", [128, 1024], BF),
-    "rb": ("sbuf", [128, 2560], BF), "rq": ("sbuf", [128, 640], CODE), "rs": ("sbuf", [128, 640], PLANE),
-    "wq": ("sbuf", [128, 256], CODE), "ws": ("sbuf", [128, 256], PLANE),
-    "qrow": ("sbuf", [128, 128], F4), "q32": ("sbuf", [128, 128], F4), "pt": ("sbuf", [128, 128], F4),
-    "fd": ("sbuf", [128, 128], F4), "j3": ("sbuf", [128, 2, 32], F4), "js": ("sbuf", [128, 2, 32], F4),
-    "ptb": ("sbuf", [128, 128], BF), "b32": ("sbuf", [128, 4], F4), "ones": ("sbuf", [128, 128], BF),
-    "zeros": ("sbuf", [128, 128], BF), "rm": ("sbuf", [128, 512], BF), "rmc": ("sbuf", [128, 96], BF),
-    "half": ("sbuf", [128, 32], F4), "big": ("sbuf", [128, 32], F4),
-    "sq": ("sbuf", [128, 640], F4), "kk": ("sbuf", [128, 640], F4), "sv": ("sbuf", [128, 128], F4),
-    "km": ("sbuf", [128, 128], F4), "kt": ("sbuf", [128, 128], F4), "kd": ("sbuf", [128, 128], F4),
-    "cm": ("sbuf", [128, 512], BF), "cs": ("sbuf", [128, 512], BF),
-    "hb": ("sbuf", [128, 2, 128], BF), "ht": ("sbuf", [128, 2, 128], BF),
-    "lbf": ("sbuf", [128, 10], F4), "lbu": ("sbuf", [128, 10], U16),
-    "bs": ("sbuf", [128, 32], F4), "pp": ("sbuf", [128, 64], F4), "pac": ("sbuf", [128, 32], F4),
-    "ff": ("sbuf", [128, 64], F4), "xm": ("sbuf", [128, 64], F4), "svb": ("sbuf", [128, 32], F4),
-    "svc": ("sbuf", [128, 32], F4), "avt": ("sbuf", [128, 32], F4), "av": ("sbuf", [128, 32], F4),
-    "avc": ("sbuf", [128, 32], F4), "af": ("sbuf", [128, 32 * 25], F4), "asum": ("sbuf", [128, 32], F4),
-    "xa": ("sbuf", [128, 32], F4), "at": ("sbuf", [128, 32], F4), "gm": ("sbuf", [128, 96], BF),
-    "gs": ("sbuf", [128, 96], F4), "hc": ("sbuf", [128, 2, 64], F4), "hd": ("sbuf", [128, 2, 64], F4),
-    "plf": ("sbuf", [128, 10], F4), "plu": ("sbuf", [128, 10], U16), "pls": ("sbuf", [128, 2], F4),
-    "pld": ("sbuf", [128, 2], F4), "lpu": ("sbuf", [128, 10], U16),
-    "zl": ("sbuf", [128, 256], F4), "zf": ("sbuf", [128, 64], F4), "yy": ("sbuf", [128, 256 * 6], F4),
-    "ps": ("psum", [128, 4096], F4),
-}
+
+
+def sb(kind, **widths):
+    return {n: ("sbuf", [128] + (w if isinstance(w, list) else [w]), kind) for n, w in widths.items()}
+
+
+SCRATCH = {"ps": ("psum", [128, 4096], F4)}
+SCRATCH.update(sb(BF, cb=512, qb=20, wb=1024, rb=2560, ptb=128, ones=128, zeros=128, rm=512, rmc=96,
+                  cm=512, cs=512, hb=[2, 128], ht=[2, 128], gm=96))
+SCRATCH.update(sb(F4, qrow=128, q32=128, pt=128, fd=128, j3=[2, 32], js=[2, 32], b32=4, half=32, big=32,
+                  sq=640, kk=640, sv=128, km=128, kt=128, kd=128, lbf=10, bs=32, pp=64, pac=32, ff=64, xm=64,
+                  svb=32, svc=32, avt=32, av=32, avc=32, af=800, asum=32, xa=32, at=32, gs=96, hc=[2, 64], hd=[2, 64],
+                  plf=10, pls=2, pld=2, zl=256, zf=64, yy=1536))
+SCRATCH.update(sb(U16, lbu=10, plu=10, lpu=10))
+SCRATCH.update(sb(CODE, rq=640, wq=256))
+SCRATCH.update(sb(PLANE, rs=640, ws=256))
 for _t in range(6):
-    SCRATCH["win%d" % _t] = ("sbuf", [128, WW[_t]], CODE)
-    SCRATCH["wis%d" % _t] = ("sbuf", [128, WW[_t]], PLANE)
+    _w = WW[_t] + (96 if _t else 0)
+    SCRATCH.update(sb(CODE, **{"win%d" % _t: _w}))
+    SCRATCH.update(sb(PLANE, **{"wis%d" % _t: _w}))
 for _t in range(5):
-    SCRATCH["out%d" % _t] = ("sbuf", [128, 32], CODE)
-    SCRATCH["ous%d" % _t] = ("sbuf", [128, 32], PLANE)
-DSEM = ["dc", "dq", "dw"] + ["dn%d" % t for t in range(1, 6)] + ["dg%d" % t for t in range(2, 5)] + ["dy%d" % t for t in range(6)]
+    SCRATCH.update(sb(CODE, **{"out%d" % _t: 32}))
+    SCRATCH.update(sb(PLANE, **{"ous%d" % _t: 128}))
+DSEM = ["dc", "dq", "dw", "do"] + ["dn%d" % t for t in range(1, 6)] + ["dg%d" % t for t in range(2, 5)] + ["dy%d" % t for t in range(6)]
 SEMAPHORES = ["cv", "ca", "ct", "cg"] + DSEM + ["arr%d" % t for t in range(5)] + ["snd%d" % t for t in range(5)]
 
 
@@ -173,19 +166,23 @@ def rank_program(g, core, T, topo):
     def PS(b, lo, hi):
         return (T.ps[:, b + lo:b + hi], [("ps", b, b + 512)])
 
-    def iota(v, pattern, mult):
-        if SCRATCH[v[1][0][0]][2] == F4:
-            op("g", lambda: g.iota(v[0], pattern, 0, mult, allow_small_or_imprecise_dtypes=True), [], v[1])
-        else:
-            op("g", lambda: g.iota(v[0], pattern, 0, mult), [], v[1])
+    def iota(v, pattern):
+        op("g", lambda: g.iota(v[0], pattern, 0, 0, allow_small_or_imprecise_dtypes=True), [], v[1])
+
+    fillers = []
+
+    def gap(k=1):
+        for _ in range(k):
+            if fillers:
+                fillers.pop(0)()
 
     dma("a", "dq", (T.qb[:, 0:20], T.qt[:, 0:20], [], [("qb", 0, 20)]))
     dma("s", "dc", (T.cb[:, 0:512], T.c[:, 0:512], [], [("cb", 0, 512)]))
     dma("s", "dw", (T.wb[:, 0:1024], T.w[:, 0:1024], [], [("wb", 0, 1024)]))
-    iota(V("qrow", 0, 128), [[1, 128]], 0)
-    iota(V("q32", 0, 128), [[0, 4], [1, 32]], 0)
+    iota(V("qrow", 0, 128), [[1, 128]])
+    iota(V("q32", 0, 128), [[0, 4], [1, 32]])
     J3, JS = (T.j3[:, :, :], [("j3", 0, 32)]), (T.js[:, :, :], [("js", 0, 32)])
-    iota(J3, [[16, 2], [0, 2], [1, 16]], 0)
+    iota(J3, [[16, 2], [0, 2], [1, 16]])
     fill(V("zeros", 0, 128), 0.0)
     fill(V("ones", 0, 128), 1.0)
     fill(V("rm", 0, 512), 1.0)
@@ -225,6 +222,7 @@ def rank_program(g, core, T, topo):
 
     def rank32(k, t):
         ts(V("km", 0, 128), k, TINY, A.max)
+        gap()
         tr(V("kt", 0, 128), V("km", 0, 128))
         tt(V("kd", 0, 128), V("km", 0, 128), V("fd", 0, 128), A.mult)
         for m in range(4):
@@ -236,53 +234,59 @@ def rank_program(g, core, T, topo):
         for m in range(4):
             u, c, d = V("kt", 32 * m, 32 * m + 1), 128 * m, 32 * m
             ts(V("cm", c + d, c + d + 32), V("kd", d, d + 32), u, A.is_lt)
+        gap()
         scan(V("cs", 0, 512), V("rm", 0, 512), V("cm", 0, 512))
+        gap()
         for m in range(4):
             ts(V3("hb", 32 * m, 32 * m + 32), J3, V("cs", 128 * m + 127, 128 * m + 128), A.is_equal,
                V("ptb", 32 * m, 32 * m + 1), A.mult)
+        gap()
         for j in range(2):
             tr(H("ht", j, 0, 128), H("hb", j, 0, 128))
         for j in range(2):
             add_up(V("lbf", 2 * t + j, 2 * t + j + 1), H("ht", j, 0, 128))
+        gap()
         cp(LB(t), V("lbf", 2 * t, 2 * t + 2))
 
     def send(t):
         d = T.cores[rank ^ [1, 2, 4, 1, 2][t]]
         rid, pid = topo.addr(d, core)
         es = topo.engines(core, d)[:8]
-        mask, n = sum(1 << e for e in es), len(es)
+        n = len(es) // 2
         a = 128 + 32 * t if t < 4 else 128
-        o, s = V("out%d" % t, 0, 32), V("ous%d" % t, 0, 32)
-        waits("g", rg(o), [])
-        g.remote_dma(T["win%d" % (t + 1)][:, a:a + 32].bitcast(dt.uint8), o[0].bitcast(dt.uint8),
-                     T.sem["arr%d" % t], T.sem["snd%d" % t], pid, rid, mask)
-        waits("g", rg(s), [])
-        g.remote_dma(T["wis%d" % (t + 1)][:, a:a + 32], s[0], T.sem["arr%d" % t], T.sem["snd%d" % t], pid, rid, mask)
+        waits("g", [("out%d" % t, 0, 32), ("ous%d" % t, 0, 128)], [])
+        to = [DstId(rid=rid, pnc=pid)]
+        g.remote_dma_fused([
+            RemoteDMATransfer(dst_ids=to, dma_engine_mask=sum(1 << e for e in es[:n]), remote_sem=T.sem["arr%d" % t],
+                              srcs=[T["out%d" % t][:, 0:32].bitcast(dt.uint8)], dsts=[T["win%d" % (t + 1)][:, a:a + 32].bitcast(dt.uint8)]),
+            RemoteDMATransfer(dst_ids=to, dma_engine_mask=sum(1 << e for e in es[n:]), remote_sem=T.sem["arr%d" % t],
+                              srcs=[T["ous%d" % t][:, 0:128]], dsts=[T["wis%d" % (t + 1)][:, a:a + 128]])],
+            local_sem=T.sem["snd%d" % t])
         ends["snd%d" % t] = ends["arr%d" % t] = 2 * n
-        for nm in ("win%d" % (t + 1), "wis%d" % (t + 1)):
-            wr.setdefault(nm, []).append((a, a + 32, "x", "arr%d" % t, 2 * n))
+        wr.setdefault("win%d" % (t + 1), []).append((a, a + 32, "x", "arr%d" % t, 2 * n))
+        wr.setdefault("wis%d" % (t + 1), []).append((a, a + 128, "x", "arr%d" % t, 2 * n))
 
     def pick(t, off):
-        o, s = V("out%d" % t, 0, 32), V("ous%d" % t, 0, 32)
         w = WW[t]
-        cp(C32(o), IX(C32(V("win%d" % t, 0, w)), off))
-        act(s, IX(V("wis%d" % t, 0, w), off), F.Copy)
+        cp(C32(V("out%d" % t, 0, 32)), IX(C32(V("win%d" % t, 0, w)), off))
+        act(V("ous%d" % t, 0, 32), IX(V("wis%d" % t, 0, w), off), F.Copy)
         send(t)
 
     def stays(t):
         pa = V("pp", 32, 64)
         act(pa, IX(V("qrow", 0, 128), LP(t - 1)), F.Copy)
         act(V("avt", 0, 32), pa, F.Identity, scale=1.0 / 256, bias=float(128 + 32 * (t - 1)))
+        fillers.append(lambda: tr(V("pac", 0, 32), pa))
+        fillers.append(lambda: tt(V("av", 0, 32), V("avt", 0, 32), V("qrow", 0, 32), A.add))
+        fillers.append(lambda: tr(V("avc", 0, 32), V("av", 0, 32)))
         rank32(KK(t), t)
-        act(V("pp", 0, 32), IX(V("qrow", 0, 128), LB(t)), F.Copy)
+        gap(9)
+        cp(V("pp", 0, 32), IX(V("qrow", 0, 128), LB(t)))
         act(V("svb", 0, 32), IX(V("sv", 0, 128), LB(t)), F.Copy)
-        tr(V("pac", 0, 32), pa)
         cp(V("bs", 0, 32), IX(V("km", 0, 128), LB(t)))
-        tt(V("av", 0, 32), V("avt", 0, 32), V("qrow", 0, 32), A.add)
         ts(V("ff", 0, 64), V("pp", 0, 64), V("pac", 0, 1), A.is_ge, PREV, A.max)
-        tt(V("xm", 0, 32), V("bs", 0, 32), V("ff", 0, 32), A.mult)
-        tr(V("avc", 0, 32), V("av", 0, 32))
         tr(V("svc", 0, 32), V("svb", 0, 32))
+        tt(V("xm", 0, 32), V("bs", 0, 32), V("ff", 0, 32), A.mult)
 
     def AF(q, t):
         i = 32 * (5 * t + q)
@@ -308,8 +312,11 @@ def rank_program(g, core, T, topo):
 
     def places(t):
         cp(V("pls", 0, 2), V("plu", 2 * t, 2 * t + 2))
+        gap()
         tt(V("pld", 0, 2), V("plf", 2 * t, 2 * t + 2), V("pls", 0, 2), A.subtract)
+        gap()
         ts(LP(t), V("pld", 0, 2), 256.0, A.mult)
+        gap()
 
     for e in range(4):
         rep(0, e, "v")
@@ -319,6 +326,7 @@ def rank_program(g, core, T, topo):
     quant("win0", "wis0", 0, 128, V("cb", 0, 512))
     b0 = mm("rq", "rs", 0, "win0", "wis0", 0)
     square(V("sq", 0, 128), b0, 0, 128)
+    dma("s", "do", *[(T["ous%d" % t][:, 32:128], T.wis0[:, 32:128], [("wis0", 32, 128)], [("ous%d" % t, 32, 128)]) for t in range(5)])
     for t in range(1, 6):
         dma("s", "dn%d" % t, *move(0, t, 0, 128))
     quant("rq", "rs", 128, 256, V("rb", 512, 1024))
@@ -327,17 +335,17 @@ def rank_program(g, core, T, topo):
     for t in range(2, 5):
         for e in range(4):
             rep(t, e, "a")
+    fillers += [lambda: ts(V("sv", 0, 128), V("qrow", 0, 128), 1.0 + 1.0 / 256, A.mult),
+                lambda: fill(V("rmc", 0, 96), 1.0),
+                lambda: fill(V("rmc", 0, 1), 0.0),
+                lambda: fill(V("rmc", 64, 65), 0.0),
+                lambda: ts(V("b32", 0, 1), V("pt", 0, 1), 32.0, A.add)]
     rank32(SQ(0), 0)
     pick(0, LB(0))
+    fillers.append(lambda: ts(JS, J3, -1.0, A.mult, V("b32", 0, 1), A.add))
     tt(KK(1), SQ(0), SQ(1), A.add)
-    ts(V("sv", 0, 128), V("qrow", 0, 128), 1.0 + 1.0 / 256, A.mult)
     scatter(KK(1), LP(0), V("big", 0, 32))
     stays(1)
-    fill(V("rmc", 0, 96), 1.0)
-    fill(V("rmc", 0, 1), 0.0)
-    fill(V("rmc", 64, 65), 0.0)
-    ts(V("b32", 0, 1), V("pt", 0, 1), 32.0, A.add)
-    ts(JS, J3, -1.0, A.mult, V("b32", 0, 1), A.add)
     quant("rq", "rs", 256, 640, V("rb", 1024, 2560))
     for t in range(2, 5):
         b = mm("rq", "rs", 128 * t, "win0", "wis0", 0)
@@ -345,28 +353,32 @@ def rank_program(g, core, T, topo):
     scatter(V("sv", 0, 128), LP(0), V("av", 0, 32))
     tt(KK(2), KK(1), SQ(2), A.add)
 
-    YB = lambda t, o: V("yy", 256 * t + 128 * o, 256 * t + 128 * o + 128)
     for t in range(1, 5):
         merge(t)
         later = [mm("rq", "rs", 128 * q, "win%d" % t, "wis%d" % t, 32 * t) for q in range(t + 1, 5)]
         if t < 4:
-            dma("s", "dg%d" % (t + 1), *move(t, t + 1, 128, 128 + 32 * t)) if t < 4 else None
+            dma("s", "dg%d" % (t + 1), *move(t, t + 1, 128, 128 + 32 * t))
         for q in range(t + 1, 5):
             square(AF(q, t - 1), later[q - t - 1], 96, 128)
         pick(t, V("plu", 2 * t, 2 * t + 2))
-        places(t)
         if t == 4:
+            places(t)
             break
-        tt(V("asum", 0, 32), AF(t, t - 1), AF(t + 1, t - 1), A.add)
-        scatter(KK(t + 1), LP(t - 1), V("asum", 0, 32))
-        scatter(KK(t + 1), LP(t), V("big", 0, 32))
-        stays(t + 1)
+        n = t + 1
+        tt(V("asum", 0, 32), AF(t, t - 1), AF(n, t - 1), A.add)
+        fillers.append(lambda: scatter(KK(n), LP(t - 1), V("asum", 0, 32)))
+        for q in range(t + 2, 5):
+            fillers.append(lambda q=q: scatter(SQ(q), LP(t - 1), AF(q, t - 1)))
+        places(t)
+        gap(9)
+        scatter(KK(n), LP(t), V("big", 0, 32))
         if t < 3:
-            for q in range(t + 2, 5):
-                scatter(SQ(q), LP(t - 1), AF(q, t - 1))
+            fillers.append(lambda: tt(KK(t + 2), KK(n), SQ(t + 2), A.add))
+        stays(n)
+        if t < 3:
             scatter(V("sv", 0, 128), LP(t), V("av", 0, 32))
-            tt(KK(t + 2), KK(t + 1), SQ(t + 2), A.add)
 
+    YB = lambda t, o: V("yy", 256 * t + 128 * o, 256 * t + 128 * o + 128)
     quant("wq", "ws", 0, 256, V("wb", 0, 1024))
     for o in range(O):
         b = mm("wq", "ws", 128 * o, "win0", "wis0", 0)

@@ -14,13 +14,14 @@ def sb(kind, **widths):
 
 
 SCRATCH = {"ps": ("psum", [128, 4096], F4)}
-SCRATCH.update(sb(BF, cb=512, qb=20, wb=1024, rb=2560, ptb=128, ones=128, zeros=128, rm=512, rmc=96,
-                  cm=512, cs=512, hb=[2, 128], ht=[2, 128], gm=96))
-SCRATCH.update(sb(F4, qrow=128, q32=128, pt=128, fd=128, j3=[2, 32], js=[2, 32], b32=4, half=32, big=32,
-                  sq=640, kk=640, sv=128, km=128, kt=128, kd=128, lbf=10, bs=32, pp=64, pac=32, ff=64, xm=64,
-                  svb=32, svc=32, avt=32, av=32, avc=32, af=800, asum=32, xa=32, at=32, gs=96, hc=[2, 64], hd=[2, 64],
-                  plf=10, pls=2, pld=2, zl=256, zf=64, yy=1536))
-SCRATCH.update(sb(U16, lbu=10, plu=10, lpu=10))
+SCRATCH.update(sb(BF, cb=512, qb=20, wb=1024, rb=2560, ptb=128, ones=128, zeros=128, rm=512, rmc=96, rmd=128,
+                  cm=512, cs=512, gd=128, gds=128, cnt=4, rv=128, vc=128, hb=[2, 128], ht=[2, 128], gm=96,
+                  hc=[2, 64], hd=[2, 64], hp=[2, 64], hq=[2, 64]))
+SCRATCH.update(sb(F4, qrow=128, q32=128, pt=128, pts=128, slr=128, fd=128, j3=[2, 32], js=[2, 32],
+                  sq=640, kk=640, sv=128, km=128, kt=128, kd=128, kf=128, fb=128, lbf=10, bs=32, bc=32, pb=32, pbc=32,
+                  pa=32, pac=32, fa=32, f2=32, xm=64, x2=32, svb=32, svc=32, af=800, asum=32, xa=32, at=32, gs=96,
+                  plf=10, lpf=10, zl=256, zf=64, yy=1536))
+SCRATCH.update(sb(U16, lbu=10, plu=10, lpx=40))
 SCRATCH.update(sb(CODE, rq=640, wq=256))
 SCRATCH.update(sb(PLANE, rs=640, ws=256))
 for _t in range(6):
@@ -99,10 +100,10 @@ def rank_program(g, core, T, topo):
         return (T[n][:, a:b] if step == 1 else T[n][:, a:b:step], [(n, a, b)])
 
     def V3(n, a, b):
-        return (T[n][:, :, a:b], [(n, a, b)])
+        return (T[n][:, :, a:b], [(n + "0", a, b), (n + "1", a, b)])
 
     def H(n, j, a, b):
-        return (T[n][:, j, a:b], [(n, a, b)])
+        return (T[n][:, j, a:b], [(n + str(j), a, b)])
 
     def IX(v, off):
         return (v[0].indirect(off[0]), v[1] + off[1])
@@ -171,6 +172,9 @@ def rank_program(g, core, T, topo):
 
     fillers = []
 
+    def later(f, *args):
+        fillers.append(lambda: f(*args))
+
     def gap(k=1):
         for _ in range(k):
             if fillers:
@@ -186,20 +190,25 @@ def rank_program(g, core, T, topo):
     fill(V("zeros", 0, 128), 0.0)
     fill(V("ones", 0, 128), 1.0)
     fill(V("rm", 0, 512), 1.0)
+    fill(V("rmd", 0, 128), 1.0)
+    fill(V("rmc", 0, 96), 1.0)
     for m in range(4):
         fill(V("rm", 128 * m, 128 * m + 1), 0.0)
+    for m in range(4):
+        fill(V("rmd", 32 * m, 32 * m + 1), 0.0)
     tr(V("pt", 0, 128), V("qrow", 0, 128))
-    cp(V("ptb", 0, 128), V("pt", 0, 128))
     ts(V("fd", 0, 128), V("q32", 0, 128), V("pt", 0, 1), A.is_ge, PREV, A.max)
-    fill(V("half", 0, 32), 2.0 ** 63)
-    tt(V("big", 0, 32), V("half", 0, 32), V("half", 0, 32), A.mult)
+    cp(V("ptb", 0, 128), V("pt", 0, 128))
 
     def rep(t, e, on):
-        o, q = V("rb", 512 * t + e, 512 * t + 512, 4), V("qb", 4 * t + e, 4 * t + e + 1)
+        o, q = (T.rb[:, 512 * t + e:512 * t + 512:4], [("rb%d" % e, t, t + 1)]), V("qb", 4 * t + e, 4 * t + e + 1)
         if on == "v":
             ts(o, V("ones", 0, 128), q, A.mult)
         else:
             act(o, V("zeros", 0, 128), F.Identity, bias=q)
+
+    def RB(t, u):
+        return (T.rb[:, 512 * t:512 * u], [("rb%d" % e, t, u) for e in range(4)])
 
     def square(dst, b, lo, hi):
         act(dst, PS(b, lo, hi), F.Square)
@@ -217,35 +226,46 @@ def rank_program(g, core, T, topo):
     def LB(t):
         return V("lbu", 2 * t, 2 * t + 2)
 
-    def LP(t):
-        return LB(0) if t == 0 else V("lpu", 2 * t, 2 * t + 2)
+    def LX(t, m):
+        return V("lpx", 8 * t + 2 * m, 8 * t + 2 * m + 2)
 
-    def rank32(k, t):
-        ts(V("km", 0, 128), k, TINY, A.max)
-        gap()
-        tr(V("kt", 0, 128), V("km", 0, 128))
-        tt(V("kd", 0, 128), V("km", 0, 128), V("fd", 0, 128), A.mult)
+    def LP(t):
+        return LX(t, 0)
+
+    KM, KT = V("km", 0, 128), V("kt", 0, 128)
+
+    def compare(k):
+        def off(ms):
+            for m in ms:
+                u, c, d = V("kt", 32 * m, 32 * m + 1), 128 * m, 32 * m
+                if m > 0:
+                    ts(V("cm", c, c + d), V("km", 0, d), u, A.is_le)
+                if m < 3:
+                    ts(V("cm", c + d + 32, c + 128), V("km", d + 32, 128), u, A.is_lt)
+
+        def diag():
+            for m in range(4):
+                c, d = 160 * m, 32 * m
+                ts(V("cm", c, c + 32), V("kd", d, d + 32), V("kt", d, d + 1), A.is_lt)
+
+        def turn():
+            tr(KT, KM)
+            tt(V("kd", 0, 128), KM, V("fd", 0, 128), A.mult)
+
+        def total():
+            scan(V("cs", 0, 512), V("rm", 0, 512), V("cm", 0, 512))
+        return [lambda: ts(KM, k, TINY, A.max), turn, lambda: off([0, 1]), lambda: off([2, 3]), diag, total]
+
+    def listed(t, cnt, val):
         for m in range(4):
-            u, c, d = V("kt", 32 * m, 32 * m + 1), 128 * m, 32 * m
-            if m > 0:
-                ts(V("cm", c, c + d), V("km", 0, d), u, A.is_le)
-            if m < 3:
-                ts(V("cm", c + d + 32, c + 128), V("km", d + 32, 128), u, A.is_lt)
-        for m in range(4):
-            u, c, d = V("kt", 32 * m, 32 * m + 1), 128 * m, 32 * m
-            ts(V("cm", c + d, c + d + 32), V("kd", d, d + 32), u, A.is_lt)
-        gap()
-        scan(V("cs", 0, 512), V("rm", 0, 512), V("cm", 0, 512))
-        gap()
-        for m in range(4):
-            ts(V3("hb", 32 * m, 32 * m + 32), J3, V("cs", 128 * m + 127, 128 * m + 128), A.is_equal,
-               V("ptb", 32 * m, 32 * m + 1), A.mult)
-        gap()
+            ts(V3("hb", 32 * m, 32 * m + 32), J3, cnt(m), A.is_equal, val(m), A.mult)
+        gap(2)
         for j in range(2):
             tr(H("ht", j, 0, 128), H("hb", j, 0, 128))
+        gap(2)
         for j in range(2):
             add_up(V("lbf", 2 * t + j, 2 * t + j + 1), H("ht", j, 0, 128))
-        gap()
+        gap(2)
         cp(LB(t), V("lbf", 2 * t, 2 * t + 2))
 
     def send(t):
@@ -272,111 +292,135 @@ def rank_program(g, core, T, topo):
         act(V("ous%d" % t, 0, 32), IX(V("wis%d" % t, 0, w), off), F.Copy)
         send(t)
 
-    def stays(t):
-        pa = V("pp", 32, 64)
-        act(pa, IX(V("qrow", 0, 128), LP(t - 1)), F.Copy)
-        act(V("avt", 0, 32), pa, F.Identity, scale=1.0 / 256, bias=float(128 + 32 * (t - 1)))
-        fillers.append(lambda: tr(V("pac", 0, 32), pa))
-        fillers.append(lambda: tt(V("av", 0, 32), V("avt", 0, 32), V("qrow", 0, 32), A.add))
-        fillers.append(lambda: tr(V("avc", 0, 32), V("av", 0, 32)))
-        rank32(KK(t), t)
+    PA, PAC = V("pa", 0, 32), V("pac", 0, 32)
+
+    def stays(t, extra=()):
+        left = len(fillers)
+        act(PA, IX(V("qrow", 0, 128), LP(t - 1)), F.Copy)
+        gap(left - 1)
+        scatter(V("rv", 0, 128), LP(t - 1), V("zeros", 0, 32))
+        tr(PAC, PA)
+        gap()
+        for x in extra:
+            later(*x)
+        cp(V("gd", 0, 128), IX(V("cm", 0, 512), V("lpx", 8 * (t - 1), 8 * t)))
+        ts(V("fb", 0, 128), V("qrow", 0, 128), V("pac", 0, 1), A.is_ge, PREV, A.max)
+        tr(V("vc", 0, 128), V("rv", 0, 128))
+        scan(V("gds", 0, 128), V("rmd", 0, 128), V("gd", 0, 128))
+        ts(V("fa", 0, 32), PA, V("pac", 0, 1), A.is_ge, PREV, A.max)
+        gap()
+        tt(V("cnt", 0, 4), V("cs", 127, 512, 128), V("gds", 31, 128, 32), A.subtract)
+        tt(V("kf", 0, 128), KM, V("fb", 0, 128), A.mult)
+        listed(t, lambda m: V("cnt", m, m + 1), lambda m: V("vc", 32 * m, 32 * m + 1))
         gap(9)
-        cp(V("pp", 0, 32), IX(V("qrow", 0, 128), LB(t)))
         act(V("svb", 0, 32), IX(V("sv", 0, 128), LB(t)), F.Copy)
-        cp(V("bs", 0, 32), IX(V("km", 0, 128), LB(t)))
-        ts(V("ff", 0, 64), V("pp", 0, 64), V("pac", 0, 1), A.is_ge, PREV, A.max)
+        cp(V("rv", 0, 128), V("qrow", 0, 128))
+        cp(V("pb", 0, 32), IX(V("qrow", 0, 128), LB(t)))
+        cp(V("bs", 0, 32), IX(KM, LB(t)))
+        cp(V("xm", 0, 32), IX(V("kf", 0, 128), LB(t)))
+        tr(V("pbc", 0, 32), V("pb", 0, 32))
+        tr(V("bc", 0, 32), V("bs", 0, 32))
         tr(V("svc", 0, 32), V("svb", 0, 32))
-        tt(V("xm", 0, 32), V("bs", 0, 32), V("ff", 0, 32), A.mult)
+        ts(V("f2", 0, 32), PA, V("pbc", 0, 1), A.is_ge, PREV, A.max)
 
     def AF(q, t):
         i = 32 * (5 * t + q)
         return V("af", i, i + 32)
 
+    def places(t, src):
+        for m in range(4):
+            ts(LX(t, m), src, float(128 * m), A.add)
+
     def merge(t):
         b = mm("rq", "rs", 128 * t, "win%d" % t, "wis%d" % t, 32 * t)
         a = AF(t, t - 1)
         square(a, b, 96, 128)
+        more = [mm("rq", "rs", 128 * q, "win%d" % t, "wis%d" % t, 32 * t) for q in range(t + 1, 5)]
+        for q in range(t + 1, 5):
+            square(AF(q, t - 1), more[q - t - 1], 96, 128)
+        if t < 4:
+            dma("s", "dg%d" % (t + 1), *move(t, t + 1, 128, 128 + 32 * t))
+            later(tt, V("asum", 0, 32), a, AF(t + 1, t - 1), A.add)
+            later(scatter, KK(t + 1), LP(t - 1), V("asum", 0, 32))
+            fillers.extend(compare(KK(t + 1)))
         ts(V("xa", 0, 32), a, TINY, A.max)
+        if t < 4:
+            scatter(V("sv", 0, 128), LP(t - 1), V("slr", 32 * (t - 1), 32 * t))
         tr(V("at", 0, 32), V("xa", 0, 32))
-        tt(V("xm", 32, 64), V("xa", 0, 32), V("ff", 32, 64), A.mult)
+        tt(V("xm", 32, 64), V("xa", 0, 32), V("fa", 0, 32), A.mult)
+        tt(V("x2", 0, 32), V("xa", 0, 32), V("f2", 0, 32), A.mult)
         ts(V("gm", 0, 64), V("xm", 0, 64), V("at", 0, 1), A.is_lt)
-        tr(V("gm", 64, 96), V("gm", 0, 32))
+        ts(V("gm", 64, 96), V("x2", 0, 32), V("bc", 0, 1), A.is_lt)
+        gap()
         scan(V("gs", 0, 96), V("rmc", 0, 96), V("gm", 0, 96))
-        ts(V3("hc", 0, 32), JS, V("gs", 95, 96), A.is_equal, V("svc", 0, 1), A.mult)
-        ts(V3("hc", 32, 64), J3, V("gs", 63, 64), A.is_equal, V("avc", 0, 1), A.mult)
+        gap()
+        s0, s1, col = V("gs", 95, 96), V("gs", 63, 64), 32 * (t - 1)
+        ts(V3("hc", 0, 32), JS, s0, A.is_equal, V("svc", 0, 1), A.mult)
+        ts(V3("hc", 32, 64), J3, s1, A.is_equal, V("pts", col, col + 1), A.mult)
+        ts(V3("hp", 0, 32), JS, s0, A.is_equal, V("pbc", 0, 1), A.mult)
+        ts(V3("hp", 32, 64), J3, s1, A.is_equal, V("pac", 0, 1), A.mult)
+        gap()
         for j in range(2):
             tr(H("hd", j, 0, 64), H("hc", j, 0, 64))
         for j in range(2):
+            tr(H("hq", j, 0, 64), H("hp", j, 0, 64))
+        gap()
+        for j in range(2):
             add_up(V("plf", 2 * t + j, 2 * t + j + 1), H("hd", j, 0, 64))
+        for j in range(2):
+            add_up(V("lpf", 2 * t + j, 2 * t + j + 1), H("hq", j, 0, 64))
+        gap()
         cp(V("plu", 2 * t, 2 * t + 2), V("plf", 2 * t, 2 * t + 2))
-
-    def places(t):
-        cp(V("pls", 0, 2), V("plu", 2 * t, 2 * t + 2))
-        gap()
-        tt(V("pld", 0, 2), V("plf", 2 * t, 2 * t + 2), V("pls", 0, 2), A.subtract)
-        gap()
-        ts(LP(t), V("pld", 0, 2), 256.0, A.mult)
-        gap()
+        places(t, V("lpf", 2 * t, 2 * t + 2))
+        pick(t, V("plu", 2 * t, 2 * t + 2))
 
     for e in range(4):
         rep(0, e, "v")
-    quant("rq", "rs", 0, 128, V("rb", 0, 512))
+    quant("win0", "wis0", 0, 128, V("cb", 0, 512))
+    quant("rq", "rs", 0, 128, RB(0, 1))
     for e in range(4):
         rep(1, e, "a")
-    quant("win0", "wis0", 0, 128, V("cb", 0, 512))
     b0 = mm("rq", "rs", 0, "win0", "wis0", 0)
     square(V("sq", 0, 128), b0, 0, 128)
     dma("s", "do", *[(T["ous%d" % t][:, 32:128], T.wis0[:, 32:128], [("wis0", 32, 128)], [("ous%d" % t, 32, 128)]) for t in range(5)])
     for t in range(1, 6):
         dma("s", "dn%d" % t, *move(0, t, 0, 128))
-    quant("rq", "rs", 128, 256, V("rb", 512, 1024))
+    quant("rq", "rs", 128, 256, RB(1, 2))
     b1 = mm("rq", "rs", 128, "win0", "wis0", 0)
     square(V("sq", 128, 256), b1, 0, 128)
     for t in range(2, 5):
         for e in range(4):
             rep(t, e, "a")
-    fillers += [lambda: ts(V("sv", 0, 128), V("qrow", 0, 128), 1.0 + 1.0 / 256, A.mult),
-                lambda: fill(V("rmc", 0, 96), 1.0),
-                lambda: fill(V("rmc", 0, 1), 0.0),
-                lambda: fill(V("rmc", 64, 65), 0.0),
-                lambda: ts(V("b32", 0, 1), V("pt", 0, 1), 32.0, A.add)]
-    rank32(SQ(0), 0)
+    later(fill, V("rmc", 0, 1), 0.0)
+    later(cp, V("rv", 0, 128), V("qrow", 0, 128))
+    later(fill, V("rmc", 64, 65), 0.0)
+    later(cp, V("sv", 0, 128), V("qrow", 0, 128))
+    later(tt, KK(1), SQ(0), SQ(1), A.add)
+    for step in compare(SQ(0)):
+        step()
+        gap()
+    fillers.extend(compare(KK(1)))
+    listed(0, lambda m: V("cs", 128 * m + 127, 128 * m + 128), lambda m: V("ptb", 32 * m, 32 * m + 1))
     pick(0, LB(0))
-    fillers.append(lambda: ts(JS, J3, -1.0, A.mult, V("b32", 0, 1), A.add))
-    tt(KK(1), SQ(0), SQ(1), A.add)
-    scatter(KK(1), LP(0), V("big", 0, 32))
-    stays(1)
-    quant("rq", "rs", 256, 640, V("rb", 1024, 2560))
+    places(0, V("lbf", 0, 2))
+    quant("rq", "rs", 256, 640, RB(2, 5))
+    stays(1, [(ts, JS, J3, V("pt", 0, 1), A.subtract),
+              (ts, V("pts", 0, 128), V("pt", 0, 128), 128.0, A.add),
+              (ts, V("slr", 0, 128), V("qrow", 0, 128), 128.0, A.add)])
     for t in range(2, 5):
         b = mm("rq", "rs", 128 * t, "win0", "wis0", 0)
         square(SQ(t), b, 0, 128)
-    scatter(V("sv", 0, 128), LP(0), V("av", 0, 32))
     tt(KK(2), KK(1), SQ(2), A.add)
 
-    for t in range(1, 5):
+    for t in range(1, 4):
         merge(t)
-        later = [mm("rq", "rs", 128 * q, "win%d" % t, "wis%d" % t, 32 * t) for q in range(t + 1, 5)]
-        if t < 4:
-            dma("s", "dg%d" % (t + 1), *move(t, t + 1, 128, 128 + 32 * t))
-        for q in range(t + 1, 5):
-            square(AF(q, t - 1), later[q - t - 1], 96, 128)
-        pick(t, V("plu", 2 * t, 2 * t + 2))
-        if t == 4:
-            places(t)
-            break
-        n = t + 1
-        tt(V("asum", 0, 32), AF(t, t - 1), AF(n, t - 1), A.add)
-        fillers.append(lambda: scatter(KK(n), LP(t - 1), V("asum", 0, 32)))
-        for q in range(t + 2, 5):
-            fillers.append(lambda q=q: scatter(SQ(q), LP(t - 1), AF(q, t - 1)))
-        places(t)
-        gap(9)
-        scatter(KK(n), LP(t), V("big", 0, 32))
+        extra = []
         if t < 3:
-            fillers.append(lambda: tt(KK(t + 2), KK(n), SQ(t + 2), A.add))
-        stays(n)
-        if t < 3:
-            scatter(V("sv", 0, 128), LP(t), V("av", 0, 32))
+            for q in range(t + 2, 5):
+                extra.append((scatter, SQ(q), LP(t - 1), AF(q, t - 1)))
+            extra.append((tt, KK(t + 2), KK(t + 1), SQ(t + 2), A.add))
+        stays(t + 1, extra)
+    merge(4)
 
     YB = lambda t, o: V("yy", 256 * t + 128 * o, 256 * t + 128 * o + 128)
     quant("wq", "ws", 0, 256, V("wb", 0, 1024))

@@ -5,7 +5,7 @@ P, K, R, O = 128, 32, 5, 2
 PREV = 1.0 - 2.0 ** -24
 TINY = 2.0 ** -121
 
-F4, BF, I32, U16, CODE, PLANE = "float32", "bfloat16", "int32", "uint16", "float8_e4m3fn_x4", "uint8"
+F4, BF, U16, CODE, PLANE = "float32", "bfloat16", "uint16", "float8_e4m3fn_x4", "uint8"
 WW = [128, 160, 192, 224, 256, 160]
 
 
@@ -14,13 +14,13 @@ def sb(kind, **widths):
 
 
 SCRATCH = {"ps": ("psum", [128, 4096], F4)}
-SCRATCH.update(sb(BF, cb=512, qb=20, wb=1024, rb=2560, ptb=128, ones=128, zeros=128, rm=512, rmc=96, rmd=128,
-                  cm=512, cs=512, gd=128, gds=128, cnt=4, rv=128, vc=128, hb=[2, 128], ht=[2, 128], gm=96,
+SCRATCH.update(sb(BF, cb=512, qb=20, wb=1024, rb=2560, ptb=128, ones=128, zeros=128, rm=512, rmc=96,
+                  cm0=512, cm1=512, cs=512, jk=640, gd=128, gds=128, rv=128, vc=128, hb=[2, 128], ht=[2, 128], gm=96,
                   hc=[2, 64], hd=[2, 64], hp=[2, 64], hq=[2, 64]))
 SCRATCH.update(sb(F4, qrow=128, q32=128, pt=128, pts=128, slr=128, fd=128, j3=[2, 32], js=[2, 32],
-                  sq=640, kk=640, sv=128, km=128, kt=128, kd=128, kf=128, fb=128, lbf=10, bs=32, bc=32, pb=32, pbc=32,
-                  pa=32, pac=32, fa=32, f2=32, xm=64, x2=32, svb=32, svc=32, af=800, asum=32, xa=32, at=32, gs=96,
-                  plf=10, lpf=10, zl=256, zf=64, yy=1536))
+                  sq=640, kk=640, sv=128, km0=128, kt0=128, kd0=128, k40=4, all0=4, km1=128, kt1=128, kd1=128, k41=4, all1=4,
+                  lbf=10, bs=32, bc=32, pb=32, pbc=32, pa=32, pac=32, fa=32, f2=32, fs=32, xm=64, x2=32, svb=32, svc=32,
+                  af=800, asum=32, xa=32, at=32, gs=96, plf=10, lpf=10, zl=256, zf=64, yy=1536))
 SCRATCH.update(sb(U16, lbu=10, plu=10, lpx=40))
 SCRATCH.update(sb(CODE, rq=640, wq=256))
 SCRATCH.update(sb(PLANE, rs=640, ws=256))
@@ -142,8 +142,8 @@ def rank_program(g, core, T, topo):
     def add_up(out, in_):
         op("v", lambda: g.vector.tensor_reduce(ap(out), ap(in_), AxisListType.X, A.add), rg(in_), rg(out))
 
-    def scan(out, d0, d1):
-        op("v", lambda: g.vector.tensor_tensor_scan(ap(out), ap(d0), ap(d1), 0.0, A.mult, A.add), rg(d0, d1), rg(out))
+    def scan(out, d0, d1, start=0.0, o=A.add):
+        op("v", lambda: g.vector.tensor_tensor_scan(ap(out), ap(d0), ap(d1), ap(start), A.mult, o), rg(d0, d1, start), rg(out))
 
     def fill(v, c):
         op("v", lambda: g.vector.memset(ap(v), c), [], rg(v))
@@ -154,6 +154,9 @@ def rank_program(g, core, T, topo):
 
     def act(out, in_, f, **kw):
         op("a", lambda: g.scalar.activation(ap(out), ap(in_), f, **{k: ap(kw[k]) for k in kw}), rg(in_, *kw.values()), rg(out))
+
+    def tally(out, in_, by):
+        op("a", lambda: g.scalar.activation(ap(by), ap(in_), F.Copy, accum_out=ap(out)), rg(in_), rg(out, by))
 
     bank = [0]
 
@@ -190,12 +193,9 @@ def rank_program(g, core, T, topo):
     fill(V("zeros", 0, 128), 0.0)
     fill(V("ones", 0, 128), 1.0)
     fill(V("rm", 0, 512), 1.0)
-    fill(V("rmd", 0, 128), 1.0)
     fill(V("rmc", 0, 96), 1.0)
     for m in range(4):
         fill(V("rm", 128 * m, 128 * m + 1), 0.0)
-    for m in range(4):
-        fill(V("rmd", 32 * m, 32 * m + 1), 0.0)
     tr(V("pt", 0, 128), V("qrow", 0, 128))
     ts(V("fd", 0, 128), V("q32", 0, 128), V("pt", 0, 1), A.is_ge, PREV, A.max)
     cp(V("ptb", 0, 128), V("pt", 0, 128))
@@ -232,40 +232,45 @@ def rank_program(g, core, T, topo):
     def LP(t):
         return LX(t, 0)
 
-    KM, KT = V("km", 0, 128), V("kt", 0, 128)
-
-    def compare(k):
-        def off(ms):
-            for m in ms:
-                u, c, d = V("kt", 32 * m, 32 * m + 1), 128 * m, 32 * m
-                if m > 0:
-                    ts(V("cm", c, c + d), V("km", 0, d), u, A.is_le)
-                if m < 3:
-                    ts(V("cm", c + d + 32, c + 128), V("km", d + 32, 128), u, A.is_lt)
-
-        def diag():
-            for m in range(4):
-                c, d = 160 * m, 32 * m
-                ts(V("cm", c, c + 32), V("kd", d, d + 32), V("kt", d, d + 1), A.is_lt)
+    def compare(t, k):
+        x = str(t % 2)
+        kn, kl = k[1][0][0], k[1][0][1]
 
         def turn():
-            tr(KT, KM)
-            tt(V("kd", 0, 128), KM, V("fd", 0, 128), A.mult)
+            tr(V("kt" + x, 0, 128), k)
+            ts(V("km" + x, 0, 128), k, TINY, A.max)
+
+        def second():
+            tt(V("kd" + x, 0, 128), V("km" + x, 0, 128), V("fd", 0, 128), A.mult)
+            ts(V("k4" + x, 0, 4), V("kt" + x, 0, 128, 32), TINY, A.max)
+
+        def run(m):
+            u, c, d = V("kt" + x, 32 * m, 32 * m + 1), 128 * m, 32 * m
+            if m > 0:
+                ts(V("cm" + x, c, c + d), V(kn, kl, kl + d), u, A.is_le)
+            if m < 3:
+                ts(V("cm" + x, c + d + 32, c + 128), V(kn, kl + d + 32, kl + 128), u, A.is_lt)
+            ts(V("cm" + x, c + d, c + d + 32), V("kd" + x, d, d + 32), V("k4" + x, m, m + 1), A.is_lt)
+            if t > 0:
+                tally(V("all" + x, m, m + 1), V("cm" + x, c, c + 128), V("jk", c, c + 128))
 
         def total():
-            scan(V("cs", 0, 512), V("rm", 0, 512), V("cm", 0, 512))
-        return [lambda: ts(KM, k, TINY, A.max), turn, lambda: off([0, 1]), lambda: off([2, 3]), diag, total]
+            scan(V("cs", 0, 512), V("rm", 0, 512), V("cm0", 0, 512))
+        return [turn, second] + [lambda m=m: run(m) for m in (1, 2, 0, 3)] + ([] if t else [total])
 
     def listed(t, cnt, val):
         for m in range(4):
             ts(V3("hb", 32 * m, 32 * m + 32), J3, cnt(m), A.is_equal, val(m), A.mult)
-        gap(2)
-        for j in range(2):
+        gap(1)
+        for j in (1, 0):
             tr(H("ht", j, 0, 128), H("hb", j, 0, 128))
-        gap(2)
-        for j in range(2):
-            add_up(V("lbf", 2 * t + j, 2 * t + j + 1), H("ht", j, 0, 128))
-        gap(2)
+        gap(1)
+        if t == 0:
+            add_up(V("lbf", 1, 2), H("ht", 1, 0, 128))
+        else:
+            tally(V("lbf", 2 * t + 1, 2 * t + 2), H("ht", 1, 0, 128), V("jk", 512, 640))
+        add_up(V("lbf", 2 * t, 2 * t + 1), H("ht", 0, 0, 128))
+        gap(1)
         cp(LB(t), V("lbf", 2 * t, 2 * t + 2))
 
     def send(t):
@@ -295,37 +300,52 @@ def rank_program(g, core, T, topo):
     PA, PAC = V("pa", 0, 32), V("pac", 0, 32)
 
     def stays(t, extra=()):
+        x = str(t % 2)
         left = len(fillers)
         act(PA, IX(V("qrow", 0, 128), LP(t - 1)), F.Copy)
         gap(left - 1)
         scatter(V("rv", 0, 128), LP(t - 1), V("zeros", 0, 32))
         tr(PAC, PA)
         gap()
-        for x in extra:
-            later(*x)
-        cp(V("gd", 0, 128), IX(V("cm", 0, 512), V("lpx", 8 * (t - 1), 8 * t)))
-        ts(V("fb", 0, 128), V("qrow", 0, 128), V("pac", 0, 1), A.is_ge, PREV, A.max)
-        tr(V("vc", 0, 128), V("rv", 0, 128))
-        scan(V("gds", 0, 128), V("rmd", 0, 128), V("gd", 0, 128))
-        ts(V("fa", 0, 32), PA, V("pac", 0, 1), A.is_ge, PREV, A.max)
+        for e in extra:
+            later(*e)
         gap()
-        tt(V("cnt", 0, 4), V("cs", 127, 512, 128), V("gds", 31, 128, 32), A.subtract)
-        tt(V("kf", 0, 128), KM, V("fb", 0, 128), A.mult)
-        listed(t, lambda m: V("cnt", m, m + 1), lambda m: V("vc", 32 * m, 32 * m + 1))
+        cp(V("gd", 0, 128), IX(V("cm" + x, 0, 512), V("lpx", 8 * (t - 1), 8 * t)))
+        tr(V("vc", 0, 128), V("rv", 0, 128))
+        for m in range(4):
+            d = 32 * m
+            scan(V("gds", d, d + 32), V("ones", 0, 32), V("gd", d, d + 32), V("all" + x, m, m + 1), A.subtract)
+        ts(V("fa", 0, 32), PA, V("pac", 0, 1), A.is_ge, PREV, A.max)
+        listed(t, lambda m: V("gds", 32 * m + 31, 32 * m + 32), lambda m: V("vc", 32 * m, 32 * m + 1))
         gap(9)
+        act(V("pb", 0, 32), IX(V("qrow", 0, 128), LB(t)), F.Copy)
         act(V("svb", 0, 32), IX(V("sv", 0, 128), LB(t)), F.Copy)
-        cp(V("rv", 0, 128), V("qrow", 0, 128))
-        cp(V("pb", 0, 32), IX(V("qrow", 0, 128), LB(t)))
-        cp(V("bs", 0, 32), IX(KM, LB(t)))
-        cp(V("xm", 0, 32), IX(V("kf", 0, 128), LB(t)))
-        tr(V("pbc", 0, 32), V("pb", 0, 32))
+        cp(V("bs", 0, 32), IX(V("km" + x, 0, 128), LB(t)))
         tr(V("bc", 0, 32), V("bs", 0, 32))
+        tr(V("pbc", 0, 32), V("pb", 0, 32))
+        ts(V("fs", 0, 32), V("pb", 0, 32), V("pac", 0, 1), A.is_ge, PREV, A.max)
         tr(V("svc", 0, 32), V("svb", 0, 32))
         ts(V("f2", 0, 32), PA, V("pbc", 0, 1), A.is_ge, PREV, A.max)
+        tt(V("xm", 0, 32), V("bs", 0, 32), V("fs", 0, 32), A.mult)
 
     def AF(q, t):
         i = 32 * (5 * t + q)
         return V("af", i, i + 32)
+
+    def YB(t, o):
+        return V("yy", 256 * t + 128 * o, 256 * t + 128 * o + 128)
+
+    def own():
+        for o in range(O):
+            b = mm("wq", "ws", 128 * o, "win0", "wis0", 0)
+            act(YB(1, o), PS(b, 0, 128), F.Copy)
+
+    def lay(t, o):
+        scatter(YB(t + 1, o), LP(t), V("zl", 128 * o + 32 * t, 128 * o + 32 * t + 32))
+        act(YB(t + 2, o), YB(t + 1, o), F.Copy)
+        if o == 1:
+            dma("s", "dy%d" % t, (T.y[:, 256 * t:256 * t + 256], T.yy[:, 256 * t + 256:256 * t + 512],
+                                  [("yy", 256 * t + 256, 256 * t + 512)], []))
 
     def places(t, src):
         for m in range(4):
@@ -340,15 +360,26 @@ def rank_program(g, core, T, topo):
             square(AF(q, t - 1), more[q - t - 1], 96, 128)
         if t < 4:
             dma("s", "dg%d" % (t + 1), *move(t, t + 1, 128, 128 + 32 * t))
+            act(V("rv", 0, 128), V("qrow", 0, 128), F.Copy)
             later(tt, V("asum", 0, 32), a, AF(t + 1, t - 1), A.add)
             later(scatter, KK(t + 1), LP(t - 1), V("asum", 0, 32))
-            fillers.extend(compare(KK(t + 1)))
+            fillers.extend(compare(t + 1, KK(t + 1)))
+        else:
+            for o in range(O):
+                b = mm("wq", "ws", 128 * o, "win4", "wis4", 128)
+                act(V("zl", 128 * o, 128 * o + 128), PS(b, 0, 128), F.Copy)
+            for u in range(4):
+                for o in range(O):
+                    for _ in range(1 if u + o else 2):
+                        later(lambda: None)
+                    later(lay, u, o)
         ts(V("xa", 0, 32), a, TINY, A.max)
         if t < 4:
             scatter(V("sv", 0, 128), LP(t - 1), V("slr", 32 * (t - 1), 32 * t))
         tr(V("at", 0, 32), V("xa", 0, 32))
         tt(V("xm", 32, 64), V("xa", 0, 32), V("fa", 0, 32), A.mult)
         tt(V("x2", 0, 32), V("xa", 0, 32), V("f2", 0, 32), A.mult)
+        gap()
         ts(V("gm", 0, 64), V("xm", 0, 64), V("at", 0, 1), A.is_lt)
         ts(V("gm", 64, 96), V("x2", 0, 32), V("bc", 0, 1), A.is_lt)
         gap()
@@ -392,14 +423,14 @@ def rank_program(g, core, T, topo):
         for e in range(4):
             rep(t, e, "a")
     later(fill, V("rmc", 0, 1), 0.0)
-    later(cp, V("rv", 0, 128), V("qrow", 0, 128))
-    later(fill, V("rmc", 64, 65), 0.0)
-    later(cp, V("sv", 0, 128), V("qrow", 0, 128))
     later(tt, KK(1), SQ(0), SQ(1), A.add)
-    for step in compare(SQ(0)):
+    later(fill, V("rmc", 64, 65), 0.0)
+    fillers.extend(compare(1, KK(1)))
+    act(V("rv", 0, 128), V("qrow", 0, 128), F.Copy)
+    act(V("sv", 0, 128), V("qrow", 0, 128), F.Copy)
+    for step in compare(0, SQ(0)):
         step()
         gap()
-    fillers.extend(compare(KK(1)))
     listed(0, lambda m: V("cs", 128 * m + 127, 128 * m + 128), lambda m: V("ptb", 32 * m, 32 * m + 1))
     pick(0, LB(0))
     places(0, V("lbf", 0, 2))
@@ -419,23 +450,14 @@ def rank_program(g, core, T, topo):
             for q in range(t + 2, 5):
                 extra.append((scatter, SQ(q), LP(t - 1), AF(q, t - 1)))
             extra.append((tt, KK(t + 2), KK(t + 1), SQ(t + 2), A.add))
+        if t == 2:
+            extra.append((quant, "wq", "ws", 0, 256, V("wb", 0, 1024)))
+        if t == 3:
+            extra.append((own,))
         stays(t + 1, extra)
     merge(4)
 
-    YB = lambda t, o: V("yy", 256 * t + 128 * o, 256 * t + 128 * o + 128)
-    quant("wq", "ws", 0, 256, V("wb", 0, 1024))
-    for o in range(O):
-        b = mm("wq", "ws", 128 * o, "win0", "wis0", 0)
-        act(YB(1, o), PS(b, 0, 128), F.Copy)
-    for o in range(O):
-        b = mm("wq", "ws", 128 * o, "win4", "wis4", 128)
-        act(V("zl", 128 * o, 128 * o + 128), PS(b, 0, 128), F.Copy)
-    for t in range(4):
-        for o in range(O):
-            scatter(YB(t + 1, o), LP(t), V("zl", 128 * o + 32 * t, 128 * o + 32 * t + 32))
-            act(YB(t + 2, o), YB(t + 1, o), F.Copy)
-        dma("s", "dy%d" % t, (T.y[:, 256 * t:256 * t + 256], T.yy[:, 256 * t + 256:256 * t + 512],
-                              [("yy", 256 * t + 256, 256 * t + 512)], []))
+    gap(99)
     bs = [mm("wq", "ws", 128 * o, "win5", "wis5", 32) for o in range(O)]
     act(V("zf", 0, 32), PS(bs[0], 96, 128), F.Copy)
     cp(V("zf", 32, 64), PS(bs[1], 96, 128))

@@ -14,14 +14,14 @@ def sb(kind, **widths):
 
 
 SCRATCH = {"ps": ("psum", [128, 4096], F4)}
-SCRATCH.update(sb(BF, cb=512, qb=20, wb=1024, rb=2560, ptb=128, ones=128, zeros=128, rm=512, rmc=96,
-                  cm0=512, cm1=512, cs=512, jk=640, gd=128, gds=128, rv=128, vc=128, hb=[2, 128], ht=[2, 128], gm=96,
+SCRATCH.update(sb(BF, cb=512, qb=20, wb=1024, rb=2560, ptb=128, ones=128, zeros=128, rmc=96, cnt=4,
+                  cm0=512, cm1=512, cs0=512, cs1=512, gj=128, rv=128, vc=128, hb=[2, 128], ht=[2, 128], gm=96,
                   hc=[2, 64], hd=[2, 64], hp=[2, 64], hq=[2, 64]))
 SCRATCH.update(sb(F4, qrow=128, q32=128, pt=128, pts=128, slr=128, fd=128, j3=[2, 32], js=[2, 32],
-                  sq=640, kk=640, sv=128, km0=128, kt0=128, kd0=128, k40=4, all0=4, km1=128, kt1=128, kd1=128, k41=4, all1=4,
-                  lbf=10, bs=32, bc=32, pb=32, pbc=32, pa=32, pac=32, fa=32, f2=32, fs=32, xm=64, x2=32, svb=32, svc=32,
-                  af=800, asum=32, xa=32, at=32, gs=96, plf=10, lpf=10, zl=256, zf=64, yy=1536))
-SCRATCH.update(sb(U16, lbu=10, plu=10, lpx=40))
+                  sq=640, kk=640, sv=128, km0=128, kt0=128, kd0=128, k40=4, km1=128, kt1=128, kd1=128, k41=4,
+                  lf=4, tf=128, tm=128, tx=32, pb=32, pbc=32, pa=32, pac=32, fa=32, xm=64, svb=32, svc=32,
+                  af=800, asum=32, xa=32, at=32, gs=96, zl=256, zf=64, yy=1536))
+SCRATCH.update(sb(U16, lbu=10, plu=10, lpu=10))
 SCRATCH.update(sb(CODE, rq=640, wq=256))
 SCRATCH.update(sb(PLANE, rs=640, ws=256))
 for _t in range(6):
@@ -139,8 +139,8 @@ def rank_program(g, core, T, topo):
     def tr(out, in_):
         op("v", lambda: g.vector.transpose(ap(out), ap(in_)), rg(in_), rg(out))
 
-    def add_up(out, in_):
-        op("v", lambda: g.vector.tensor_reduce(ap(out), ap(in_), AxisListType.X, A.add), rg(in_), rg(out))
+    def most(out, in_):
+        op("v", lambda: g.vector.tensor_reduce(ap(out), ap(in_), AxisListType.X, A.max), rg(in_), rg(out))
 
     def scan(out, d0, d1, start=0.0, o=A.add):
         op("v", lambda: g.vector.tensor_tensor_scan(ap(out), ap(d0), ap(d1), ap(start), A.mult, o), rg(d0, d1, start), rg(out))
@@ -153,10 +153,9 @@ def rank_program(g, core, T, topo):
         op("v", lambda: g.vector.quantize_mx(x[0], y[0], ap(in_)), rg(in_), rg(x, y))
 
     def act(out, in_, f, **kw):
-        op("a", lambda: g.scalar.activation(ap(out), ap(in_), f, **{k: ap(kw[k]) for k in kw}), rg(in_, *kw.values()), rg(out))
-
-    def tally(out, in_, by):
-        op("a", lambda: g.scalar.activation(ap(by), ap(in_), F.Copy, accum_out=ap(out)), rg(in_), rg(out, by))
+        more = [kw["accum_out"]] if "accum_out" in kw else []
+        op("a", lambda: g.scalar.activation(ap(out), ap(in_), f, **{k: ap(kw[k]) for k in kw}),
+           rg(in_, *[kw[k] for k in kw if k != "accum_out"]), rg(out, *more))
 
     bank = [0]
 
@@ -192,10 +191,7 @@ def rank_program(g, core, T, topo):
     iota(J3, [[16, 2], [0, 2], [1, 16]])
     fill(V("zeros", 0, 128), 0.0)
     fill(V("ones", 0, 128), 1.0)
-    fill(V("rm", 0, 512), 1.0)
     fill(V("rmc", 0, 96), 1.0)
-    for m in range(4):
-        fill(V("rm", 128 * m, 128 * m + 1), 0.0)
     tr(V("pt", 0, 128), V("qrow", 0, 128))
     ts(V("fd", 0, 128), V("q32", 0, 128), V("pt", 0, 1), A.is_ge, PREV, A.max)
     cp(V("ptb", 0, 128), V("pt", 0, 128))
@@ -226,11 +222,8 @@ def rank_program(g, core, T, topo):
     def LB(t):
         return V("lbu", 2 * t, 2 * t + 2)
 
-    def LX(t, m):
-        return V("lpx", 8 * t + 2 * m, 8 * t + 2 * m + 2)
-
     def LP(t):
-        return LX(t, 0)
+        return V("lpu" if t else "lbu", 2 * t, 2 * t + 2)
 
     def compare(t, k):
         x = str(t % 2)
@@ -251,27 +244,21 @@ def rank_program(g, core, T, topo):
             if m < 3:
                 ts(V("cm" + x, c + d + 32, c + 128), V(kn, kl + d + 32, kl + 128), u, A.is_lt)
             ts(V("cm" + x, c + d, c + d + 32), V("kd" + x, d, d + 32), V("k4" + x, m, m + 1), A.is_lt)
-            if t > 0:
-                tally(V("all" + x, m, m + 1), V("cm" + x, c, c + 128), V("jk", c, c + 128))
 
         def total():
-            scan(V("cs", 0, 512), V("rm", 0, 512), V("cm0", 0, 512))
-        return [turn, second] + [lambda m=m: run(m) for m in (1, 2, 0, 3)] + ([] if t else [total])
+            for m in (1, 2, 0, 3):
+                scan(V("cs" + x, 128 * m, 128 * m + 128), V("ones", 0, 128), V("cm" + x, 128 * m, 128 * m + 128))
+        return [turn, second] + [lambda m=m: run(m) for m in (1, 2, 0, 3)] + [total]
 
     def listed(t, cnt, val):
         for m in range(4):
             ts(V3("hb", 32 * m, 32 * m + 32), J3, cnt(m), A.is_equal, val(m), A.mult)
-        gap(1)
+        gap()
         for j in (1, 0):
             tr(H("ht", j, 0, 128), H("hb", j, 0, 128))
-        gap(1)
-        if t == 0:
-            add_up(V("lbf", 1, 2), H("ht", 1, 0, 128))
-        else:
-            tally(V("lbf", 2 * t + 1, 2 * t + 2), H("ht", 1, 0, 128), V("jk", 512, 640))
-        add_up(V("lbf", 2 * t, 2 * t + 1), H("ht", 0, 0, 128))
-        gap(1)
-        cp(LB(t), V("lbf", 2 * t, 2 * t + 2))
+        gap()
+        for j in (1, 0):
+            most(V("lbu", 2 * t + j, 2 * t + j + 1), H("ht", j, 0, 128))
 
     def send(t):
         d = T.cores[rank ^ [1, 2, 4, 1, 2][t]]
@@ -299,6 +286,21 @@ def rank_program(g, core, T, topo):
 
     PA, PAC = V("pa", 0, 32), V("pac", 0, 32)
 
+    def AF(q, t):
+        i = 32 * (5 * t + q)
+        return V("af", i, i + 32)
+
+    def head(t):
+        b = mm("rq", "rs", 128 * t, "win%d" % t, "wis%d" % t, 32 * t)
+        square(AF(t, t - 1), b, 96, 128)
+
+    def floor(t):
+        ts(V("xa", 0, 32), AF(t, t - 1), TINY, A.max)
+
+    def turned():
+        tr(V("at", 0, 32), V("xa", 0, 32))
+        tt(V("xm", 32, 64), V("xa", 0, 32), V("fa", 0, 32), A.mult)
+
     def stays(t, extra=()):
         x = str(t % 2)
         left = len(fillers)
@@ -307,30 +309,32 @@ def rank_program(g, core, T, topo):
         scatter(V("rv", 0, 128), LP(t - 1), V("zeros", 0, 32))
         tr(PAC, PA)
         gap()
+        for m in range(4):
+            act(V("gj", 32 * m, 32 * m + 32), IX(V("cm" + x, 128 * m, 128 * m + 128), LP(t - 1)), F.Copy, accum_out=V("lf", m, m + 1))
         for e in extra:
             later(*e)
-        gap()
-        cp(V("gd", 0, 128), IX(V("cm" + x, 0, 512), V("lpx", 8 * (t - 1), 8 * t)))
         tr(V("vc", 0, 128), V("rv", 0, 128))
-        for m in range(4):
-            d = 32 * m
-            scan(V("gds", d, d + 32), V("ones", 0, 32), V("gd", d, d + 32), V("all" + x, m, m + 1), A.subtract)
+        ts(V("tf", 0, 128), V("qrow", 0, 128), V("pac", 0, 1), A.is_ge, PREV, A.max)
+        gap()
         ts(V("fa", 0, 32), PA, V("pac", 0, 1), A.is_ge, PREV, A.max)
-        listed(t, lambda m: V("gds", 32 * m + 31, 32 * m + 32), lambda m: V("vc", 32 * m, 32 * m + 1))
-        gap(9)
+        tt(V("tm", 0, 128), V("km" + x, 0, 128), V("tf", 0, 128), A.mult)
+        tt(V("cnt", 0, 4), V("cs" + x, 127, 512, 128), V("lf", 0, 4), A.subtract)
+        gap()
+        listed(t, lambda m: V("cnt", m, m + 1), lambda m: V("vc", 32 * m, 32 * m + 1))
+        gap()
+        if t > 1:
+            head(t)
         act(V("pb", 0, 32), IX(V("qrow", 0, 128), LB(t)), F.Copy)
         act(V("svb", 0, 32), IX(V("sv", 0, 128), LB(t)), F.Copy)
-        cp(V("bs", 0, 32), IX(V("km" + x, 0, 128), LB(t)))
-        tr(V("bc", 0, 32), V("bs", 0, 32))
+        cp(V("xm", 0, 32), IX(V("tm", 0, 128), LB(t)))
+        if t > 1:
+            floor(t)
+        gap(9)
+        tr(V("tx", 0, 32), V("xm", 0, 32))
+        if t > 1:
+            turned()
         tr(V("pbc", 0, 32), V("pb", 0, 32))
-        ts(V("fs", 0, 32), V("pb", 0, 32), V("pac", 0, 1), A.is_ge, PREV, A.max)
         tr(V("svc", 0, 32), V("svb", 0, 32))
-        ts(V("f2", 0, 32), PA, V("pbc", 0, 1), A.is_ge, PREV, A.max)
-        tt(V("xm", 0, 32), V("bs", 0, 32), V("fs", 0, 32), A.mult)
-
-    def AF(q, t):
-        i = 32 * (5 * t + q)
-        return V("af", i, i + 32)
 
     def YB(t, o):
         return V("yy", 256 * t + 128 * o, 256 * t + 128 * o + 128)
@@ -347,14 +351,10 @@ def rank_program(g, core, T, topo):
             dma("s", "dy%d" % t, (T.y[:, 256 * t:256 * t + 256], T.yy[:, 256 * t + 256:256 * t + 512],
                                   [("yy", 256 * t + 256, 256 * t + 512)], []))
 
-    def places(t, src):
-        for m in range(4):
-            ts(LX(t, m), src, float(128 * m), A.add)
-
     def merge(t):
-        b = mm("rq", "rs", 128 * t, "win%d" % t, "wis%d" % t, 32 * t)
         a = AF(t, t - 1)
-        square(a, b, 96, 128)
+        if t == 1:
+            head(t)
         more = [mm("rq", "rs", 128 * q, "win%d" % t, "wis%d" % t, 32 * t) for q in range(t + 1, 5)]
         for q in range(t + 1, 5):
             square(AF(q, t - 1), more[q - t - 1], 96, 128)
@@ -373,15 +373,15 @@ def rank_program(g, core, T, topo):
                     for _ in range(1 if u + o else 2):
                         later(lambda: None)
                     later(lay, u, o)
-        ts(V("xa", 0, 32), a, TINY, A.max)
+        if t == 1:
+            floor(t)
         if t < 4:
             scatter(V("sv", 0, 128), LP(t - 1), V("slr", 32 * (t - 1), 32 * t))
-        tr(V("at", 0, 32), V("xa", 0, 32))
-        tt(V("xm", 32, 64), V("xa", 0, 32), V("fa", 0, 32), A.mult)
-        tt(V("x2", 0, 32), V("xa", 0, 32), V("f2", 0, 32), A.mult)
+        if t == 1:
+            turned()
+        tt(V("gm", 64, 96), V("xa", 0, 32), V("tx", 0, 32), A.is_le)
         gap()
         ts(V("gm", 0, 64), V("xm", 0, 64), V("at", 0, 1), A.is_lt)
-        ts(V("gm", 64, 96), V("x2", 0, 32), V("bc", 0, 1), A.is_lt)
         gap()
         scan(V("gs", 0, 96), V("rmc", 0, 96), V("gm", 0, 96))
         gap()
@@ -397,12 +397,10 @@ def rank_program(g, core, T, topo):
             tr(H("hq", j, 0, 64), H("hp", j, 0, 64))
         gap()
         for j in range(2):
-            add_up(V("plf", 2 * t + j, 2 * t + j + 1), H("hd", j, 0, 64))
+            most(V("plu", 2 * t + j, 2 * t + j + 1), H("hd", j, 0, 64))
         for j in range(2):
-            add_up(V("lpf", 2 * t + j, 2 * t + j + 1), H("hq", j, 0, 64))
+            most(V("lpu", 2 * t + j, 2 * t + j + 1), H("hq", j, 0, 64))
         gap()
-        cp(V("plu", 2 * t, 2 * t + 2), V("plf", 2 * t, 2 * t + 2))
-        places(t, V("lpf", 2 * t, 2 * t + 2))
         pick(t, V("plu", 2 * t, 2 * t + 2))
 
     for e in range(4):
@@ -431,9 +429,8 @@ def rank_program(g, core, T, topo):
     for step in compare(0, SQ(0)):
         step()
         gap()
-    listed(0, lambda m: V("cs", 128 * m + 127, 128 * m + 128), lambda m: V("ptb", 32 * m, 32 * m + 1))
+    listed(0, lambda m: V("cs0", 128 * m + 127, 128 * m + 128), lambda m: V("ptb", 32 * m, 32 * m + 1))
     pick(0, LB(0))
-    places(0, V("lbf", 0, 2))
     quant("rq", "rs", 256, 640, RB(2, 5))
     stays(1, [(ts, JS, J3, V("pt", 0, 1), A.subtract),
               (ts, V("pts", 0, 128), V("pt", 0, 128), 128.0, A.add),

from concourse.bass import DstId, RemoteDMATransfer
from concourse.mybir import dt, AluOpType, AxisListType, ActivationFunctionType

P, K, R, O = 128, 32, 5, 2
PREV = 1.0 - 2.0 ** -24
TINY = 2.0 ** -121

F4, BF, U16, CODE, PLANE = "float32", "bfloat16", "uint16", "float8_e4m3fn_x4", "uint8"
WW = [128, 160, 192, 224, 256, 160]


def sb(kind, **widths):
    return {n: ("sbuf", [128] + (w if isinstance(w, list) else [w]), kind) for n, w in widths.items()}


SCRATCH = {"ps": ("psum", [128, 4096], F4)}
SCRATCH.update(sb(BF, cb=512, qb=20, wb=1024, rb=2560, ptb=128, ones=128, zeros=128, rmc=96, cnt=4,
                  cm0=512, cm1=512, cs0=512, cs1=512, gj=128, rv=128, vc=128, hb=[2, 128], ht=[2, 128], gm=96,
                  hc=[2, 64], hd=[2, 64], hp=[2, 64], hq=[2, 64]))
SCRATCH.update(sb(F4, qrow=128, q32=128, pt=128, pts=128, slr=128, fd=128, j3=[2, 32], js=[2, 32],
                  sq=640, kk=640, sv=128, km0=128, kt0=128, kd0=128, k40=4, km1=128, kt1=128, kd1=128, k41=4,
                  lf=4, tf=128, tm=128, tx=32, pb=32, pbc=32, pa=32, pac=32, fa=32, xm=64, svb=32, svc=32,
                  af=800, asum=32, xa=32, at=32, gs=96, zl=256, zf=64, yy=1536))
SCRATCH.update(sb(U16, lbu=10, plu=10, lpu=10))
SCRATCH.update(sb(CODE, rq=640, wq=256))
SCRATCH.update(sb(PLANE, rs=640, ws=256))
for _t in range(6):
    _w = WW[_t] + (96 if _t else 0)
    SCRATCH.update(sb(CODE, **{"win%d" % _t: _w}))
    SCRATCH.update(sb(PLANE, **{"wis%d" % _t: _w}))
for _t in range(5):
    SCRATCH.update(sb(CODE, **{"out%d" % _t: 32}))
    SCRATCH.update(sb(PLANE, **{"ous%d" % _t: 128}))
DSEM = ["dc", "dq", "dw", "do"] + ["dn%d" % t for t in range(1, 6)] + ["dg%d" % t for t in range(2, 5)] + ["dy%d" % t for t in range(6)]
SEMAPHORES = ["cv", "ca", "ct", "cg"] + DSEM + ["arr%d" % t for t in range(5)] + ["snd%d" % t for t in range(5)]


def rank_program(g, core, T, topo):
    rank = T.rank_of(core)
    if rank is None:
        return
    A, F = AluOpType, ActivationFunctionType
    eng = {"v": g.vector, "a": g.scalar, "t": g.tensor, "g": g, "s": g.sync}
    csem = {"v": "cv", "a": "ca", "t": "ct", "g": "cg"}
    count = {"v": 0, "a": 0, "t": 0, "g": 0}
    known = {q: {} for q in eng}
    snap = {}
    wr, rd = {}, {}
    ends = {}

    def wait(q, sem, val):
        if known[q].get(sem, 0) >= val:
            return
        eng[q].wait_ge(T.sem[sem], val)
        known[q][sem] = val
        for s, v in snap.get((sem, val), {}).items():
            if known[q].get(s, 0) < v:
                known[q][s] = v

    def waits(q, reads, writes):
        need = {}
        for (n, lo, hi) in reads:
            for (l, h, q2, s, v) in wr.get(n, ()):
                if l < hi and lo < h:
                    need[s] = max(need.get(s, 0), v)
        for (n, lo, hi) in writes:
            for (l, h, q2, s, v) in wr.get(n, ()):
                if l < hi and lo < h:
                    need[s] = max(need.get(s, 0), v)
            for (l, h, q2, s, v) in rd.get(n, ()):
                if l < hi and lo < h and (q2 != q or s[0] == "d"):
                    need[s] = max(need.get(s, 0), v)
        for s in sorted(need):
            wait(q, s, need[s])

    def note(q, reads, writes, sem, val):
        snap[(sem, val)] = dict(known[q])
        for (n, lo, hi) in writes:
            wr[n] = [e for e in wr.get(n, ()) if not (lo <= e[0] and e[1] <= hi)] + [(lo, hi, q, sem, val)]
            rd[n] = [e for e in rd.get(n, ()) if not (lo <= e[0] and e[1] <= hi)]
        for (n, lo, hi) in reads:
            rd.setdefault(n, []).append((lo, hi, q, sem, val))

    def op(q, fn, reads, writes):
        waits(q, reads, writes)
        ins = fn()
        count[q] += 1
        ins.then_inc(T.sem[csem[q]], 1)
        note(q, reads, writes, csem[q], count[q])

    def dma(q, sem, *moves):
        for (out, in_, reads, writes) in moves:
            waits(q, reads, writes)
            eng[q].dma_start(out, in_).then_inc(T.sem[sem], 16)
        ends[sem] = 16 * len(moves)
        for (out, in_, reads, writes) in moves:
            note(q, reads, writes, sem, ends[sem])

    def V(n, a, b, step=1):
        return (T[n][:, a:b] if step == 1 else T[n][:, a:b:step], [(n, a, b)])

    def V3(n, a, b):
        return (T[n][:, :, a:b], [(n + "0", a, b), (n + "1", a, b)])

    def H(n, j, a, b):
        return (T[n][:, j, a:b], [(n + str(j), a, b)])

    def IX(v, off):
        return (v[0].indirect(off[0]), v[1] + off[1])

    def C32(v):
        return (v[0].bitcast(dt.uint32), v[1])

    def ap(x):
        return x[0] if isinstance(x, tuple) else x

    def rg(*xs):
        r = []
        for x in xs:
            if isinstance(x, tuple):
                r += x[1]
        return r

    def ts(out, i0, s1, op0, s2=None, op1=None):
        if op1 is None:
            op("v", lambda: g.vector.tensor_scalar(ap(out), ap(i0), ap(s1), None, op0), rg(i0, s1), rg(out))
        else:
            op("v", lambda: g.vector.tensor_scalar(ap(out), ap(i0), ap(s1), ap(s2), op0, op1), rg(i0, s1, s2), rg(out))

    def tt(out, i0, i1, o):
        op("v", lambda: g.vector.tensor_tensor(ap(out), ap(i0), ap(i1), o), rg(i0, i1), rg(out))

    def cp(out, in_):
        op("v", lambda: g.vector.tensor_copy(ap(out), ap(in_)), rg(in_), rg(out))

    def scatter(win, off, vals):
        op("v", lambda: g.vector.tensor_copy(win[0].indirect(off[0]), ap(vals)), rg(off, vals), rg(win))

    def tr(out, in_):
        op("v", lambda: g.vector.transpose(ap(out), ap(in_)), rg(in_), rg(out))

    def most(out, in_):
        op("v", lambda: g.vector.tensor_reduce(ap(out), ap(in_), AxisListType.X, A.max), rg(in_), rg(out))

    def scan(out, d0, d1, start=0.0, o=A.add):
        op("v", lambda: g.vector.tensor_tensor_scan(ap(out), ap(d0), ap(d1), ap(start), A.mult, o), rg(d0, d1, start), rg(out))

    def fill(v, c):
        op("v", lambda: g.vector.memset(ap(v), c), [], rg(v))

    def quant(q, s, a, b, in_):
        x, y = V(q, a, b), V(s, a, b)
        op("v", lambda: g.vector.quantize_mx(x[0], y[0], ap(in_)), rg(in_), rg(x, y))

    def act(out, in_, f, **kw):
        more = [kw["accum_out"]] if "accum_out" in kw else []
        op("a", lambda: g.scalar.activation(ap(out), ap(in_), f, **{k: ap(kw[k]) for k in kw}),
           rg(in_, *[kw[k] for k in kw if k != "accum_out"]), rg(out, *more))

    bank = [0]

    def mm(lq, ls, la, rq, rs, ra):
        b = 512 * (bank[0] % 8)
        bank[0] += 1
        l, m, r, s = V(lq, la, la + 128), V(ls, la, la + 128), V(rq, ra, ra + 128), V(rs, ra, ra + 128)
        op("t", lambda: g.tensor.matmul_mx(T.ps[:, b:b + 128], l[0], m[0], r[0], s[0], True, True), rg(l, m, r, s), [("ps", b, b + 512)])
        return b

    def PS(b, lo, hi):
        return (T.ps[:, b + lo:b + hi], [("ps", b, b + 512)])

    def iota(v, pattern):
        op("g", lambda: g.iota(v[0], pattern, 0, 0, allow_small_or_imprecise_dtypes=True), [], v[1])

    fillers = []

    def later(f, *args):
        fillers.append(lambda: f(*args))

    def gap(k=1):
        for _ in range(k):
            if fillers:
                fillers.pop(0)()

    dma("a", "dq", (T.qb[:, 0:20], T.qt[:, 0:20], [], [("qb", 0, 20)]))
    dma("s", "dc", (T.cb[:, 0:512], T.c[:, 0:512], [], [("cb", 0, 512)]))
    dma("s", "dw", (T.wb[:, 0:1024], T.w[:, 0:1024], [], [("wb", 0, 1024)]))
    iota(V("qrow", 0, 128), [[1, 128]])
    iota(V("q32", 0, 128), [[0, 4], [1, 32]])
    J3, JS = (T.j3[:, :, :], [("j3", 0, 32)]), (T.js[:, :, :], [("js", 0, 32)])
    iota(J3, [[16, 2], [0, 2], [1, 16]])
    fill(V("zeros", 0, 128), 0.0)
    fill(V("ones", 0, 128), 1.0)
    fill(V("rmc", 0, 96), 1.0)
    tr(V("pt", 0, 128), V("qrow", 0, 128))
    ts(V("fd", 0, 128), V("q32", 0, 128), V("pt", 0, 1), A.is_ge, PREV, A.max)
    cp(V("ptb", 0, 128), V("pt", 0, 128))

    def rep(t, e, on):
        o, q = (T.rb[:, 512 * t + e:512 * t + 512:4], [("rb%d" % e, t, t + 1)]), V("qb", 4 * t + e, 4 * t + e + 1)
        if on == "v":
            ts(o, V("ones", 0, 128), q, A.mult)
        else:
            act(o, V("zeros", 0, 128), F.Identity, bias=q)

    def RB(t, u):
        return (T.rb[:, 512 * t:512 * u], [("rb%d" % e, t, u) for e in range(4)])

    def square(dst, b, lo, hi):
        act(dst, PS(b, lo, hi), F.Square)

    def move(m, n, a, b):
        x, y, s, r = V("win%d" % n, a, b), V("win%d" % m, a, b), V("wis%d" % n, a, b), V("wis%d" % m, a, b)
        return ((x[0].bitcast(dt.uint8), y[0].bitcast(dt.uint8), y[1], x[1]), (s[0], r[0], r[1], s[1]))

    def SQ(t):
        return V("sq", 128 * t, 128 * t + 128)

    def KK(t):
        return V("kk", 128 * t, 128 * t + 128)

    def LB(t):
        return V("lbu", 2 * t, 2 * t + 2)

    def LP(t):
        return V("lpu" if t else "lbu", 2 * t, 2 * t + 2)

    def compare(t, k):
        x = str(t % 2)
        kn, kl = k[1][0][0], k[1][0][1]

        def turn():
            tr(V("kt" + x, 0, 128), k)
            ts(V("km" + x, 0, 128), k, TINY, A.max)

        def second():
            tt(V("kd" + x, 0, 128), V("km" + x, 0, 128), V("fd", 0, 128), A.mult)
            ts(V("k4" + x, 0, 4), V("kt" + x, 0, 128, 32), TINY, A.max)

        def run(m):
            u, c, d = V("kt" + x, 32 * m, 32 * m + 1), 128 * m, 32 * m
            if m > 0:
                ts(V("cm" + x, c, c + d), V(kn, kl, kl + d), u, A.is_le)
            if m < 3:
                ts(V("cm" + x, c + d + 32, c + 128), V(kn, kl + d + 32, kl + 128), u, A.is_lt)
            ts(V("cm" + x, c + d, c + d + 32), V("kd" + x, d, d + 32), V("k4" + x, m, m + 1), A.is_lt)

        def total():
            for m in (1, 2, 0, 3):
                scan(V("cs" + x, 128 * m, 128 * m + 128), V("ones", 0, 128), V("cm" + x, 128 * m, 128 * m + 128))
        return [turn, second] + [lambda m=m: run(m) for m in (1, 2, 0, 3)] + [total]

    def listed(t, cnt, val):
        for m in range(4):
            ts(V3("hb", 32 * m, 32 * m + 32), J3, cnt(m), A.is_equal, val(m), A.mult)
        gap()
        for j in (1, 0):
            tr(H("ht", j, 0, 128), H("hb", j, 0, 128))
        gap()
        for j in (1, 0):
            most(V("lbu", 2 * t + j, 2 * t + j + 1), H("ht", j, 0, 128))

    def send(t):
        d = T.cores[rank ^ [1, 2, 4, 1, 2][t]]
        rid, pid = topo.addr(d, core)
        es = topo.engines(core, d)[:8]
        n = len(es) // 2
        a = 128 + 32 * t if t < 4 else 128
        waits("g", [("out%d" % t, 0, 32), ("ous%d" % t, 0, 128)], [])
        to = [DstId(rid=rid, pnc=pid)]
        g.remote_dma_fused([
            RemoteDMATransfer(dst_ids=to, dma_engine_mask=sum(1 << e for e in es[:n]), remote_sem=T.sem["arr%d" % t],
                              srcs=[T["out%d" % t][:, 0:32].bitcast(dt.uint8)], dsts=[T["win%d" % (t + 1)][:, a:a + 32].bitcast(dt.uint8)]),
            RemoteDMATransfer(dst_ids=to, dma_engine_mask=sum(1 << e for e in es[n:]), remote_sem=T.sem["arr%d" % t],
                              srcs=[T["ous%d" % t][:, 0:128]], dsts=[T["wis%d" % (t + 1)][:, a:a + 128]])],
            local_sem=T.sem["snd%d" % t])
        ends["snd%d" % t] = ends["arr%d" % t] = 2 * n
        wr.setdefault("win%d" % (t + 1), []).append((a, a + 32, "x", "arr%d" % t, 2 * n))
        wr.setdefault("wis%d" % (t + 1), []).append((a, a + 128, "x", "arr%d" % t, 2 * n))

    def pick(t, off):
        w = WW[t]
        cp(C32(V("out%d" % t, 0, 32)), IX(C32(V("win%d" % t, 0, w)), off))
        act(V("ous%d" % t, 0, 32), IX(V("wis%d" % t, 0, w), off), F.Copy)
        send(t)

    PA, PAC = V("pa", 0, 32), V("pac", 0, 32)

    def AF(q, t):
        i = 32 * (5 * t + q)
        return V("af", i, i + 32)

    def head(t):
        b = mm("rq", "rs", 128 * t, "win%d" % t, "wis%d" % t, 32 * t)
        square(AF(t, t - 1), b, 96, 128)

    def floor(t):
        ts(V("xa", 0, 32), AF(t, t - 1), TINY, A.max)

    def turned():
        tr(V("at", 0, 32), V("xa", 0, 32))
        tt(V("xm", 32, 64), V("xa", 0, 32), V("fa", 0, 32), A.mult)

    def stays(t, extra=()):
        x = str(t % 2)
        left = len(fillers)
        act(PA, IX(V("qrow", 0, 128), LP(t - 1)), F.Copy)
        gap(left - 1)
        scatter(V("rv", 0, 128), LP(t - 1), V("zeros", 0, 32))
        tr(PAC, PA)
        gap()
        for m in range(4):
            act(V("gj", 32 * m, 32 * m + 32), IX(V("cm" + x, 128 * m, 128 * m + 128), LP(t - 1)), F.Copy, accum_out=V("lf", m, m + 1))
        for e in extra:
            later(*e)
        tr(V("vc", 0, 128), V("rv", 0, 128))
        ts(V("tf", 0, 128), V("qrow", 0, 128), V("pac", 0, 1), A.is_ge, PREV, A.max)
        gap()
        ts(V("fa", 0, 32), PA, V("pac", 0, 1), A.is_ge, PREV, A.max)
        tt(V("tm", 0, 128), V("km" + x, 0, 128), V("tf", 0, 128), A.mult)
        tt(V("cnt", 0, 4), V("cs" + x, 127, 512, 128), V("lf", 0, 4), A.subtract)
        gap()
        listed(t, lambda m: V("cnt", m, m + 1), lambda m: V("vc", 32 * m, 32 * m + 1))
        gap()
        if t > 1:
            head(t)
        act(V("pb", 0, 32), IX(V("qrow", 0, 128), LB(t)), F.Copy)
        act(V("svb", 0, 32), IX(V("sv", 0, 128), LB(t)), F.Copy)
        cp(V("xm", 0, 32), IX(V("tm", 0, 128), LB(t)))
        if t > 1:
            floor(t)
        gap(9)
        tr(V("tx", 0, 32), V("xm", 0, 32))
        if t > 1:
            turned()
        tr(V("pbc", 0, 32), V("pb", 0, 32))
        tr(V("svc", 0, 32), V("svb", 0, 32))

    def YB(t, o):
        return V("yy", 256 * t + 128 * o, 256 * t + 128 * o + 128)

    def own():
        for o in range(O):
            b = mm("wq", "ws", 128 * o, "win0", "wis0", 0)
            act(YB(1, o), PS(b, 0, 128), F.Copy)

    def lay(t, o):
        scatter(YB(t + 1, o), LP(t), V("zl", 128 * o + 32 * t, 128 * o + 32 * t + 32))
        act(YB(t + 2, o), YB(t + 1, o), F.Copy)
        if o == 1:
            dma("s", "dy%d" % t, (T.y[:, 256 * t:256 * t + 256], T.yy[:, 256 * t + 256:256 * t + 512],
                                  [("yy", 256 * t + 256, 256 * t + 512)], []))

    def merge(t):
        a = AF(t, t - 1)
        if t == 1:
            head(t)
        more = [mm("rq", "rs", 128 * q, "win%d" % t, "wis%d" % t, 32 * t) for q in range(t + 1, 5)]
        for q in range(t + 1, 5):
            square(AF(q, t - 1), more[q - t - 1], 96, 128)
        if t < 4:
            dma("s", "dg%d" % (t + 1), *move(t, t + 1, 128, 128 + 32 * t))
            act(V("rv", 0, 128), V("qrow", 0, 128), F.Copy)
            later(tt, V("asum", 0, 32), a, AF(t + 1, t - 1), A.add)
            later(scatter, KK(t + 1), LP(t - 1), V("asum", 0, 32))
            fillers.extend(compare(t + 1, KK(t + 1)))
        else:
            for o in range(O):
                b = mm("wq", "ws", 128 * o, "win4", "wis4", 128)
                act(V("zl", 128 * o, 128 * o + 128), PS(b, 0, 128), F.Copy)
            for u in range(4):
                for o in range(O):
                    for _ in range(1 if u + o else 2):
                        later(lambda: None)
                    later(lay, u, o)
        if t == 1:
            floor(t)
        if t < 4:
            scatter(V("sv", 0, 128), LP(t - 1), V("slr", 32 * (t - 1), 32 * t))
        if t == 1:
            turned()
        tt(V("gm", 64, 96), V("xa", 0, 32), V("tx", 0, 32), A.is_le)
        gap()
        ts(V("gm", 0, 64), V("xm", 0, 64), V("at", 0, 1), A.is_lt)
        gap()
        scan(V("gs", 0, 96), V("rmc", 0, 96), V("gm", 0, 96))
        gap()
        s0, s1, col = V("gs", 95, 96), V("gs", 63, 64), 32 * (t - 1)
        ts(V3("hc", 0, 32), JS, s0, A.is_equal, V("svc", 0, 1), A.mult)
        ts(V3("hc", 32, 64), J3, s1, A.is_equal, V("pts", col, col + 1), A.mult)
        ts(V3("hp", 0, 32), JS, s0, A.is_equal, V("pbc", 0, 1), A.mult)
        ts(V3("hp", 32, 64), J3, s1, A.is_equal, V("pac", 0, 1), A.mult)
        gap()
        for j in range(2):
            tr(H("hd", j, 0, 64), H("hc", j, 0, 64))
        for j in range(2):
            tr(H("hq", j, 0, 64), H("hp", j, 0, 64))
        gap()
        for j in range(2):
            most(V("plu", 2 * t + j, 2 * t + j + 1), H("hd", j, 0, 64))
        for j in range(2):
            most(V("lpu", 2 * t + j, 2 * t + j + 1), H("hq", j, 0, 64))
        gap()
        pick(t, V("plu", 2 * t, 2 * t + 2))

    for e in range(4):
        rep(0, e, "v")
    quant("win0", "wis0", 0, 128, V("cb", 0, 512))
    quant("rq", "rs", 0, 128, RB(0, 1))
    for e in range(4):
        rep(1, e, "a")
    b0 = mm("rq", "rs", 0, "win0", "wis0", 0)
    square(V("sq", 0, 128), b0, 0, 128)
    dma("s", "do", *[(T["ous%d" % t][:, 32:128], T.wis0[:, 32:128], [("wis0", 32, 128)], [("ous%d" % t, 32, 128)]) for t in range(5)])
    for t in range(1, 6):
        dma("s", "dn%d" % t, *move(0, t, 0, 128))
    quant("rq", "rs", 128, 256, RB(1, 2))
    b1 = mm("rq", "rs", 128, "win0", "wis0", 0)
    square(V("sq", 128, 256), b1, 0, 128)
    for t in range(2, 5):
        for e in range(4):
            rep(t, e, "a")
    later(fill, V("rmc", 0, 1), 0.0)
    later(tt, KK(1), SQ(0), SQ(1), A.add)
    later(fill, V("rmc", 64, 65), 0.0)
    fillers.extend(compare(1, KK(1)))
    act(V("rv", 0, 128), V("qrow", 0, 128), F.Copy)
    act(V("sv", 0, 128), V("qrow", 0, 128), F.Copy)
    for step in compare(0, SQ(0)):
        step()
        gap()
    listed(0, lambda m: V("cs0", 128 * m + 127, 128 * m + 128), lambda m: V("ptb", 32 * m, 32 * m + 1))
    pick(0, LB(0))
    quant("rq", "rs", 256, 640, RB(2, 5))
    stays(1, [(ts, JS, J3, V("pt", 0, 1), A.subtract),
              (ts, V("pts", 0, 128), V("pt", 0, 128), 128.0, A.add),
              (ts, V("slr", 0, 128), V("qrow", 0, 128), 128.0, A.add)])
    for t in range(2, 5):
        b = mm("rq", "rs", 128 * t, "win0", "wis0", 0)
        square(SQ(t), b, 0, 128)
    tt(KK(2), KK(1), SQ(2), A.add)

    for t in range(1, 4):
        merge(t)
        extra = []
        if t < 3:
            for q in range(t + 2, 5):
                extra.append((scatter, SQ(q), LP(t - 1), AF(q, t - 1)))
            extra.append((tt, KK(t + 2), KK(t + 1), SQ(t + 2), A.add))
        if t == 2:
            extra.append((quant, "wq", "ws", 0, 256, V("wb", 0, 1024)))
        if t == 3:
            extra.append((own,))
        stays(t + 1, extra)
    merge(4)

    gap(99)
    bs = [mm("wq", "ws", 128 * o, "win5", "wis5", 32) for o in range(O)]
    act(V("zf", 0, 32), PS(bs[0], 96, 128), F.Copy)
    cp(V("zf", 32, 64), PS(bs[1], 96, 128))
    for o in range(O):
        scatter(YB(5, o), LP(4), V("zf", 32 * o, 32 * o + 32))
        dma("s" if o == 0 else "a", "dy%d" % (4 + o), (T.y[:, 1024 + 128 * o:1152 + 128 * o],
            T.yy[:, 1280 + 128 * o:1408 + 128 * o], YB(5, o)[1], []))
    for q in ("v", "a", "t", "g"):
        wait("g", csem[q], count[q])
    for s in sorted(ends):
        wait("g", s, ends[s])
